import numpy as np, ml_dtypes
CORES = [66,74,82,90,194,202,210,218]
N = 8
BF = ml_dtypes.bfloat16
V, VB, S, L, LB, B, RO = 2048, 11, 1024, 128, 32, 4, 5
def picks(lm, s, j):
    g = np.arange(8)[:, None, None]; k = np.arange(16)[None, :, None]
    a = lm[g, k, s[:, None, :]] >> VB
    return lm[g, (j[:, None, :] + k) & 15, a] & (V - 1)
def sample(f, lm, x, p, q, s, t):
    g = np.arange(8)[:, None, None, None]; i = np.arange(16)[None, :, None, None]; k = np.arange(16)[None, :, None]
    j = (np.sum(x, axis=1) + t) & 15
    m = picks(lm, s, j)
    void = np.any(m[:, :, None, :] == q[:, None, :, :], axis=2)
    n = np.where((p >= 0) & (((j[:, None, :] + k) & 1) == 1), p, np.where(void, -1, m))
    fz = f[g, i, np.maximum(n, 0)[:, None, :, :]]
    dist = np.where(n < 0, 1 << 20, np.sum(np.abs(fz - x[:, :, None, :]), axis=1))
    return j, n, dist, np.argmin(dist, axis=1)
def names(rng, pop, share, n):
    i = rng.integers(0, 64, (N, 8, 16, n)); g = np.arange(8).reshape(1, 8, 1, 1)
    return np.where(rng.random(i.shape) < share, pop[g, i], rng.integers(0, V, i.shape))
def parts(rng, share=0.5, fp=0.5, fq=0.6):
    pop = rng.integers(0, V, (8, 64)); d = {}
    d["f"] = rng.integers(0, 256, (N, 8, 16, V)); d["lm"] = rng.integers(0, S, (N, 8, 16, S)) * V + names(rng, pop, share, S)
    d["sn"] = rng.integers(0, S, (N, 8, V)); d["th"] = rng.integers(500, 1200, (N, 8, L)); d["x"] = rng.integers(0, 256, (N, 8, 16, L))
    d["p"] = np.where(rng.random((N, 8, 16, L)) < fp, names(rng, pop, share, L), -1)
    d["q"] = np.where(rng.random((N, 8, 16, L)) < fq, names(rng, pop, share, L), -1)
    d["s"] = rng.integers(0, S, (N, 8, L)); d["v"] = rng.integers(0, V, (N, 8, L))
    return d
def pack(d):
    o = {"feat": d["f"].reshape(N, 128, V).astype(np.float32).astype(BF), "lm": d["lm"].reshape(N, 128, S).astype(np.int32), "sn": d["sn"].astype(np.int32), "th": d["th"].astype(np.int32),
         "lx": d["x"].reshape(N, 128, L).astype(np.float32).astype(BF), "lp": d["p"].reshape(N, 128, L).astype(np.int32), "lq": d["q"].reshape(N, 128, L).astype(np.int32),
         "ls": d["s"].astype(np.int32), "lv": d["v"].astype(np.int32)}
    return {k: np.ascontiguousarray(a) for k, a in o.items()}
def setup_inputs(rng):
    return pack(parts(rng))
def setup_inputs_spread(rng):
    d = parts(rng, share=rng.choice(np.array([0.0, 0.3, 0.7, 0.95]), (N, 8, 1, 1)), fp=rng.random((N, 8, 1, L)), fq=rng.random((N, 8, 1, L)))
    d["f"] = np.minimum((np.exp2(8 * rng.random((N, 8, 1, V))) * rng.random((N, 8, 16, V))).astype(np.int64), 255)
    d["x"] = np.minimum((np.exp2(8 * rng.random((N, 8, 1, L))) * rng.random((N, 8, 16, L))).astype(np.int64), 255)
    d["th"] = np.minimum(np.exp2(12 * rng.random((N, 8, L))).astype(np.int64), 4095)
    d["lm"] = np.minimum((S * rng.random((N, 8, 16, S)) ** 4).astype(np.int64), S - 1) * V + (d["lm"] & (V - 1))
    d["sn"] = np.minimum((S * rng.random((N, 8, V)) ** 3).astype(np.int64), S - 1)
    d["s"] = np.minimum((S * rng.random((N, 8, L)) ** 2).astype(np.int64), S - 1)
    return pack(d)
def twoends(rng, lo, hi, *shape):
    share = np.array([1.0, 0.7, 1.0, 0.7, 0.9, 0.7, 0.8, 1.0]).reshape((1, 8) + (1,) * (len(shape) - 2))
    return np.where(rng.random(shape) < share, np.where(rng.random(shape) < 0.5, lo, hi), rng.integers(lo, hi + 1, shape))
def byrecord(rng, lo, hi, n):
    c = rng.integers(0, 4, (N, 8, 1, n))
    return np.where(c == 0, lo, np.where(c == 1, hi, twoends(rng, lo, hi, N, 8, 16, n)))
def setup_inputs_ends(rng):
    d = {"f": byrecord(rng, 0, 255, V), "x": byrecord(rng, 0, 255, L), "p": byrecord(rng, -1, V - 1, L), "q": byrecord(rng, -1, V - 1, L), "lm": twoends(rng, 0, S * V - 1, N, 8, 16, S),
         "sn": twoends(rng, 0, S - 1, N, 8, V), "th": twoends(rng, 0, 4095, N, 8, L), "s": twoends(rng, 0, S - 1, N, 8, L), "v": twoends(rng, 0, V - 1, N, 8, L)}
    r = N - 1
    d["f"][r, 7, :, 0] = 255; d["f"][r, 7, :, V - 1] = 255; d["x"][r, 7, :, 0::2] = 255; d["x"][r, 7, :, 1::2] = 0
    d["th"][r, 7, 1::4] = 4095; d["th"][r, 7, L - 1] = 4095; d["sn"][r, 7, 0] = 0; d["sn"][r, 7, V - 1] = S - 1
    d["s"][r, 7, L - 1] = 0; d["p"][r, 7, :, L - 1] = -1; d["q"][r, 7, :, L - 1] = -1
    d["lm"][r, 7, 0, 0] = S * V - 1; d["lm"][r, 7, 0, S - 1] = S * V - 1; d["lm"][r, 7, 15, 0] = 0
    d["sn"][0, 6:] = S - 1; d["s"][0, 6:] = 0; d["th"][0, 6:] = 4095; d["q"][0, 6:] = -1; d["s"][0, 6, L - 1] = S - 1
    return pack(d)
def setup_inputs_corners(rng):
    d = parts(rng)
    u = rng.random((N, 8, 16, S)); w = rng.random((N, 8, 16, S)); c = np.arange(S)
    link = np.where(u < 0.2, c, np.where(u < 0.3, 0, np.where(u < 0.4, S - 1, d["lm"] >> VB)))
    d["lm"] = link * V + np.where(w < 0.05, 0, np.where(w < 0.1, V - 1, d["lm"] & (V - 1)))
    u = rng.random((N, 8, L)); d["s"] = np.where(u < 0.05, 0, np.where(u < 0.1, S - 1, d["s"]))
    u = rng.random((N, 8, L)); d["v"] = np.where(u < 0.05, 0, np.where(u < 0.1, V - 1, d["v"]))
    k = np.arange(16)[None, :, None]
    for r in range(N):
        m = picks(d["lm"][r], d["s"][r], np.sum(d["x"][r], axis=1) & 15)
        kind = rng.integers(0, 7, (8, 1, L)); kind[:, 0, :7] = np.arange(7); kind[:, 0, L - 7:] = np.arange(7)[::-1]
        o = rng.integers(0, 16, (8, 1, L)); keep = np.take_along_axis(m, o, 1); full = rng.integers(0, V, (8, 16, L))
        p, q = d["p"][r], d["q"][r]
        p = np.where((kind == 0) | (kind == 1) | (kind == 3), -1, np.where(kind == 2, full, np.where(kind == 4, np.where(k == o, full, -1), np.where(kind == 5, m[:, ::-1], p))))
        q = np.where((kind == 0) | (kind == 2), m, np.where(kind == 1, np.where(m == keep, -1, m), np.where(kind == 3, -1, np.where((kind == 4) | (kind == 5), full[::-1], q))))
        d["p"][r] = p; d["q"][r] = q
        j, n, dist, best = sample(d["f"][r], d["lm"][r], d["x"][r], p, q, d["s"][r], 0)
        nb = np.take_along_axis(n, best[:, None, :], 1)[:, 0]; db = np.take_along_axis(dist, best[:, None, :], 1)[:, 0]
        e = rng.integers(0, 6, (8, L))
        d["th"][r] = np.minimum(np.where(e == 0, db, np.where(e == 1, db + 1, np.where(e == 2, 0, np.where(e == 3, 4095, d["th"][r])))), 4095)
        gi, li = np.nonzero((nb >= 0) & (rng.random((8, L)) < 0.1))
        d["sn"][r][gi, nb[gi, li]] = d["s"][r][gi, li]
    d["lm"][:, 5] = (d["lm"][:, 5] >> VB) * V + 7; d["v"][:, 5] = 7; d["p"][:, 5] = -1; d["th"][:, 5] = 4095
    d["q"][:, 5] = 7; d["q"][:, 5, :, :31] = -1; d["sn"][:, 5, 7] = 10 + np.arange(N); d["s"][:, 5, :31] = 100
    return pack(d)
def setup_inputs_crowd(rng):
    d = parts(rng)
    d["f"][:, 1::2] = np.tile(rng.integers(0, 256, (N, 8, 16, 16)), V >> 4)[:, 1::2]
    d["sn"][:, 1::2] = np.take_along_axis(rng.integers(0, S, (N, 8, 2)), rng.integers(0, 2, (N, 8, V)), 2)[:, 1::2]
    c = np.stack([rng.permutation(S)[:N] for g in range(8)], axis=1); c[:, 6] = c[0, 6]
    a = (100 + np.arange(N) % 3)[:, None, None]
    for g in (0, 2, 4, 6):
        d["sn"][:, g] = c[:, g, None]; d["s"][:, g] = (c[:, g, None] + 1 + rng.integers(0, S - 1, (N, L))) % S
        d["q"][:, g] = -1; d["th"][:, g] = 4095
        if g < 4: d["f"][:, g] = a; d["x"][:, g] = a; d["th"][:, g] = 1
        if g == 2 or g == 4:
            pos = rng.integers(0, L, N); pos[N - 1] = L - 1; d["s"][np.arange(N), g, pos] = c[:, g]
    return pack(d)
def setup_inputs_turns(rng):
    d = parts(rng)
    base = rng.integers(0, 100, (8, 16)); base[:, 0] ^= 1 - (np.sum(base, axis=1) & 1)
    lev = np.stack([6 * rng.permutation(N) for g in range(8)], axis=1) + rng.integers(0, 14, 8) + 100 * (np.arange(N) & 1)[:, None]
    d["f"][:] = (base + lev[:, :, None])[..., None]; d["x"][:] = (base + lev[:, :, None])[..., None]
    c = rng.choice(np.array([0, 1, 31, L - 1, L]), (N, 8)); c[0] = L; c[N - 1] = L - 1
    for r in range(N):
        for g in range(8):
            z = rng.permutation(V)[:L]; u = rng.permutation(S)[:L]; go = rng.permutation(L) < c[r, g]
            d["sn"][r, g, z] = u; d["p"][r, g, 0] = z
            d["s"][r, g] = np.where(go, (u + 1 + rng.integers(0, S - 1, L)) % S, u)
    h = 1 + np.arange(L) // LB; rr = np.arange(N)[:, None]; here = lev[:, :, None]
    one = lev[(rr - h) % N].transpose(0, 2, 1); two = lev[(rr - 2 * h) % N].transpose(0, 2, 1)
    d1 = 16 * np.abs(here - one); d2 = 16 * np.abs(here - ((one + two) >> 1)); e = rng.integers(0, 2, (N, 8, L))
    d["th"] = d1 - (c[:, :, None] & 31) + e
    calm = np.where((d2 > 0) & (d2 + 32 <= d1), d2 + e, 1)
    for g in (1, 6): d["th"][:, g] = calm[:, g]
    return pack(d)
def check_inputs(d):
    bad = []
    for k, lo, hi in (("feat", 0, 255), ("lm", 0, S * V - 1), ("sn", 0, S - 1), ("th", 0, 4095), ("lx", 0, 255), ("lp", -1, V - 1), ("lq", -1, V - 1), ("ls", 0, S - 1), ("lv", 0, V - 1)):
        a = np.asarray(d[k]).astype(np.float64)
        if not np.all((a >= lo) & (a <= hi) & (np.floor(a) == a)): bad.append("range of " + k)
    return bad
def reference(feat, lm, sn, th, lx, lp, lq, ls, lv):
    f = feat.astype(np.float32).astype(np.int64).reshape(N, 8, 16, V); rec = lm.astype(np.int64).reshape(N, 8, 16, S)
    sup = sn.astype(np.int64); thr = th.astype(np.int64)
    x = lx.astype(np.float32).astype(np.int64).reshape(N, 8, 16, L); p = lp.astype(np.int64).reshape(N, 8, 16, L); q = lq.astype(np.int64).reshape(N, 8, 16, L)
    s = ls.astype(np.int64); v = lv.astype(np.int64); moved = np.zeros((N, 8), np.int64)
    g2 = np.arange(8)[:, None]; g3 = np.arange(8)[:, None, None]; i3 = np.arange(16)[None, :, None]
    for t in range(RO):
        for r in range(N):
            j, n, dist, best = sample(f[r], rec[r], x[r], p[r], q[r], s[r], t)
            nb = np.take_along_axis(n, best[:, None, :], 1)[:, 0]; db = np.take_along_axis(dist, best[:, None, :], 1)[:, 0]
            live = nb >= 0; z = np.maximum(nb, 0); s2 = sup[r][g2, z]
            go = live & (db < thr[r] + (moved[r][:, None] & 31)) & (s2 != s[r])
            m2 = picks(rec[r], s2, j)
            eq = n[:, :, None, :] == m2[:, None, :, :]
            p[r] = np.where(go[:, None, :], np.where(np.any(eq, axis=2), -1, n), p[r])
            q[r] = np.where(go[:, None, :], np.where(np.any(eq, axis=1), -1, m2), q[r])
            for g in range(8):
                w = np.flatnonzero(go[g]); u, first = np.unique(s2[g, w], return_index=True); w = w[first]
                rec[r, g, j[g, w], u] = s[r, g, w] * V + v[r, g, w]
            x[r] = np.where(live[:, None, :], (x[r] + f[r][g3, i3, z[:, None, :]]) >> 1, x[r])
            s[r] = np.where(go, s2, s[r]); moved[r] = np.sum(go, axis=1)
        if t < RO - 1:
            for b in range(B):
                lo, hi = b * LB, (b + 1) * LB
                for a in (x, p, q, s, v): a[..., lo:hi] = np.roll(a[..., lo:hi], 1 + b, axis=0)
    return {"ylm": rec.reshape(N, 128, S).astype(np.float32), "yx": x.reshape(N, 128, L).astype(np.float32), "yp": p.reshape(N, 128, L).astype(np.float32),
            "yq": q.reshape(N, 128, L).astype(np.float32), "ys": s.astype(np.float32)}

@@ -1,0 +1,635 @@
+import math
+from concourse.bass import DstId, RemoteDMATransfer
+from concourse.mybir import dt, AluOpType, AxisListType, ActivationFunctionType
+
+N, RO = 8, 5
+NFS = (5, 2)
+FX, FS, FV, FR, FW, FP, FM = range(7)
+ABS = (0, 0)
+GV = ((0, 0, 0), (8, 0, 0))
+ZV, ZG = 3840, 3072
+ZW = 16384 + 128
+PA = 0
+FWV = 0
+SEED, NOISE, GRAIN = 1, 0.0, 0.04
+BIAS = [0.5, -1.0, 1.75, -0.75, 0, 3.0, -0.25, 0.75, -0.5, 0.0, 0, 6, -0.5, -1.5, 1, -1.5, 4]
+SYNC, TRAVEL, GC, SEND = 0.1, 2.5, 1.56, 0.5
+
+POOL = {"b": 19456, "h": 3072, "f": 7168, "i": 5632, "u": 1024}
+SCRATCH = {
+    "zt": ("sbuf", [128, ZW], "bfloat16"),
+    "rt": ("sbuf", [128, 1152], "float32"),
+    "fd": ("sbuf", [128, 2304], "bfloat16"),
+    "fw": ("sbuf", [128, 2304], "bfloat16"),
+    "sx": ("sbuf", [128, 2304], "int32"),
+    "pb": ("sbuf", [128, POOL["b"]], "bfloat16"),
+    "ph": ("sbuf", [128, POOL["h"]], "float16"),
+    "pf": ("sbuf", [128, POOL["f"]], "float32"),
+    "pi": ("sbuf", [128, POOL["i"]], "int32"),
+    "pu": ("sbuf", [128, POOL["u"]], "uint16"),
+}
+for _t in range(RO):
+    for _e in range(2):
+        SCRATCH["lin%d_%d" % (_t, _e)] = ("sbuf", [128, 128 * NFS[_e]], "float16")
+        SCRATCH["lout%d_%d" % (_t, _e)] = ("sbuf", [128, 128 * NFS[_e]], "float16")
+for _k in range(8):
+    SCRATCH["ps%d" % _k] = ("psum", [128, 512], "float32")
+NDMA = 24
+SEMAPHORES = (["cV", "cA", "cP", "cG", "sent"] + ["arr%d_%d_%d" % (t, h, e) for t in range(1, RO) for h in range(2) for e in range(2)]
+              + ["d%d" % k for k in range(NDMA)])
+
+A = AluOpType
+AF = ActivationFunctionType
+WIDTH = {"zt": 2, "fd": 2, "fw": 2, "pb": 2, "ph": 2, "pu": 2}
+
+
+def vw(buf, c0, n, cs=1, p0=0, p1=128, ps=1):
+    return (buf, p0, p1, ps, c0, n, cs)
+
+
+def sub(v, a, n, cs=1):
+    return (v[0], v[1], v[2], v[3], v[4] + a * v[6], n, v[6] * cs)
+
+
+def prt(v, p0, p1, ps=1):
+    return (v[0], p0, p1, ps, v[4], v[5], v[6])
+
+
+def ind(win, off):
+    return ("ind", win, off)
+
+
+def isv(x):
+    return isinstance(x, tuple)
+
+
+def cnt(v):
+    return v[2][5] * 16 if v[0] == "ind" else v[5]
+
+
+def two(v):
+    b = v[1][0] if v[0] == "ind" else v[0]
+    return b in WIDTH or b[:3] in ("lin", "lou")
+
+
+def psum(v):
+    return v[0][:2] == "ps"
+
+
+def build():
+    ops = []
+    cur = [14]
+    top = {"b": 0, "h": 0, "f": 0, "i": 0, "u": 0}
+
+    def al(k, n):
+        c0 = top[k]
+        top[k] = c0 + (n + 15) // 16 * 16
+        assert top[k] <= POOL[k], k
+        return vw("p" + k, c0, n)
+
+    def regs(vs):
+        o = []
+        for v in vs:
+            if not isv(v):
+                continue
+            if v[0] == "ind":
+                o += regs([v[1], v[2]])
+            else:
+                o.append((v[0], v[4], v[4] + (v[5] - 1) * v[6] + 1, v[6]))
+        return o
+
+    def add(q, k, a, rd, wr, c, lat=0.0):
+        r = regs(rd)
+        w = []
+        for v in wr:
+            if v[0] == "ind":
+                w += regs([v[1]]); r += regs([v[2]])
+            else:
+                w += regs([v])
+        ops.append({"q": q, "k": k, "a": a, "r": r, "w": w, "c": c, "lat": lat, "x": [], "h": cur[0]})
+        return len(ops) - 1
+
+    def vc(out, ins, tt=False):
+        n = cnt(out)
+        if out[0] == "ind":
+            return 0.05 + n * 3.8 * 0.00104
+        if ins[0][0] == "ind":
+            return 0.05 + n * GC * 0.00104
+        f = 1.0
+        if tt and not any(psum(v) for v in ins):
+            f = 2.0
+        elif not tt and two(out) and all(two(v) for v in ins):
+            f = 0.5
+        return max(64, n * f) * 0.00104
+
+    def cp(o, i): return add("V", "cp", (o, i), [i], [o], vc(o, [i]))
+    def tt(o, a, b, op): return add("V", "tt", (o, a, b, op), [a, b], [o], vc(o, [a, b], True))
+    def ts(o, a, s1, op0, s2=None, op1=None): return add("V", "ts", (o, a, s1, s2, op0, op1), [a, s1, s2], [o], vc(o, [a]))
+    def scan(o, d0, d1, init, op0, op1): return add("V", "scan", (o, d0, d1, init, op0, op1), [d0, d1], [o], vc(o, [d0, d1]))
+    def vtr(o, i): return add("V", "vtr", (o, i), [i], [o], vc(o, [i]))
+    def red(o, i, op): return add("V", "red", (o, i, op), [i], [o], max(64, cnt(i)) * 0.00104)
+    def ms(o, c): return add("V", "ms", (o, c), [], [o], vc(o, [o]))
+    def act(o, i, f, scale=1.0, bias=0.0, acc=None):
+        n = cnt(o)
+        return add("A", "act", (o, i, f, scale, bias, acc), [i, scale], [o] if acc is None else [o, acc], 0.065 + n * GC * 0.00104 if i[0] == "ind" else max(64, n) * 0.00104)
+    def mm(o, l, r, st, sp):
+        return add("P", "mm", (o, l, r, st, sp), [l, r], [o], max(64, cnt(r)) * 0.00052 * (1 if two(r) else 4))
+    def iota(o, pat, base, ch): return add("G", "iota", (o, pat, base, ch), [], [o], 0.13 + cnt(o) * 0.0021)
+    def asel(o, i, pat, op, fill, base, ch): return add("G", "asel", (o, i, pat, op, fill, base, ch), [i], [o], 0.17 + cnt(o) * 0.0021)
+    def dma(q, prs, lat):
+        rd = [i for o, i in prs if i[0][0] != "@"]; wr = [o for o, i in prs if o[0][0] != "@"]
+        return add(q, "dma", prs, rd, wr, 0.06 * len(prs), lat)
+
+    ZT, RT = vw("zt", 0, ZW), vw("rt", 0, 1152)
+    FD, FWT, SX = vw("fd", 0, 2304), vw("fw", 0, 2304), vw("sx", 0, 2304)
+    PS = [vw("ps%d" % k, 0, 512) for k in range(8)]
+
+    def fld(buf, f, l0, n):
+        e = 0 if f < NFS[0] else 1
+        return vw("%s_%d" % (buf, e), l0 * NFS[e] + f - e * NFS[0], n, NFS[e])
+    def rec(buf, e, l0): return vw("%s_%d" % (buf, e), l0 * NFS[e], 64 * NFS[e])
+
+    lmi = al("i", 1024); lpi = al("i", 128); lqi = al("i", 128); sm8 = al("i", 384); lxb = al("b", 128)
+    dma("S", [(lmi, ("@lm", 0, 128, 1, 0, 1024))], 3.0)
+    dma("S", [(lxb, ("@lx", 0, 128, 1, 0, 128)), (lpi, ("@lp", 0, 128, 1, 0, 128)), (lqi, ("@lq", 0, 128, 1, 0, 128))], 2.5)
+    dma("A", [(prt(sub(sm8, 128 * k, 128), 0, 8), ("@" + nm, 0, 8, 1, 0, 128)) for k, nm in enumerate(("ls", "th", "lv"))], 2.5)
+    dma("S", [(sub(FD, 0, 2048), ("@feat", 0, 128, 1, 0, 2048))], 4.5)
+
+    ones = al("b", 160); ms(ones, 1.0)
+    ipad = al("b", 160); asel(ipad, ones, [[-1, 160]], A.is_equal, 0.0, 16, 1)
+    ib = sub(ipad, 16, 128)
+    pi_ = al("i", 16); iota(sub(pi_, 0, 1), [[0, 1]], 0, 1)
+    col = al("f", 16)
+    def c_(k): return sub(col, k, 1)
+    ts(sub(pi_, 1, 1), sub(pi_, 0, 1), 15, A.bitwise_and); cp(c_(0), sub(pi_, 1, 1))
+    ts(sub(pi_, 2, 1), sub(pi_, 0, 1), 7, A.bitwise_and); ts(c_(1), sub(pi_, 2, 1), 2048.0, A.mult)
+    ts(sub(pi_, 5, 1), sub(pi_, 0, 1), 16, A.bitwise_and); ts(c_(3), sub(pi_, 5, 1), 0.0625, A.mult)
+    ts(c_(4), c_(3), -1.0, A.mult, 1.0, A.add)
+    ts(sub(pi_, 6, 1), sub(pi_, 0, 1), 4, A.arith_shift_right); cp(c_(5), sub(pi_, 6, 1))
+    ts(sub(pi_, 7, 1), sub(pi_, 0, 1), 1, A.bitwise_and); cp(c_(6), sub(pi_, 7, 1))
+    ts(c_(7), sub(pi_, 2, 1), 0.0, A.is_equal)
+    ts(c_(8), sub(pi_, 1, 1), 4096.0, A.mult, 4096.0, A.add); ts(c_(9), sub(pi_, 1, 1), 1024.0, A.mult)
+    cp(c_(10), sub(pi_, 0, 1))
+    mg = al("f", 128); iota(mg, [[1, 8], [0, 16]], 0, 0)
+    mk = al("f", 128); iota(mk, [[0, 8], [1, 16]], 0, 0)
+    mpar = al("f", 128); iota(mpar, [[0, 64], [1, 2]], 0, 0)
+    selff = al("f", 128); iota(selff, [[2, 128]], 2048, 0)
+    dw = al("f", 16); iota(dw, [[15360, 2], [16, 8]], 1024, 0)
+    e8 = al("f", 128); e8lo = al("f", 128); e8hi = al("f", 128)
+    bo = al("b", 128); ts(bo, mg, c_(5), A.is_equal)
+    boh = al("h", 128); cp(boh, bo)
+    boc = al("b", 128); act(boc, bo, AF.Copy, -65536.0)
+    ts(prt(e8, 0, 8), prt(mg, 0, 8), prt(c_(10), 0, 8), A.is_equal)
+    t8 = al("f", 128); ts(prt(t8, 0, 8), prt(mk, 0, 8), 8.0, A.is_ge)
+    tt(prt(e8hi, 0, 8), prt(e8, 0, 8), prt(t8, 0, 8), A.mult); tt(prt(e8lo, 0, 8), prt(e8, 0, 8), prt(e8hi, 0, 8), A.subtract)
+    sw3 = al("b", 3 * 144); ms(sw3, 0.0)
+    for k, sc in enumerate((1.0, 131072.0, -65536.0)):
+        act(sub(sw3, 144 * k + 16, 8, 16), sub(bo, 0, 8, 16), AF.Copy, sc)
+    def sel(s, k): return sub(sw3, 144 * s + 16 - k, 128)
+    diag = al("f", 128); ts(diag, mk, c_(0), A.is_equal)
+    seg0 = al("f", 128); ts(seg0, mk, 0.0, A.not_equal)
+    segb = al("f", 64); ts(segb, sub(mk, 0, 64), 0.0, A.is_equal, 1e12, A.mult)
+    selfh = al("h", 128); cp(selfh, selff)
+    selfy = al("f", 128); vtr(selfy, selff)
+    i4k = al("b", 128); act(i4k, ib, AF.Copy, 4096.0)
+    ineg = al("b", 128)
+    if any(ABS): act(ineg, ib, AF.Copy, -1.0)
+    dk = al("b", 128); act(dk, ib, AF.Identity, c_(8))
+    i4n = al("b", 128); act(i4n, ib, AF.Copy, -4096.0)
+    ic = al("b", 128); act(ic, ib, AF.Copy, -65536.0)
+    m8 = al("b", 128); m8t = al("b", 128); mk8 = al("f", 128); iota(mk8, [[0, 16], [2048, 8]], 0, 0)
+    ts(m8t, mk8, c_(1), A.is_equal); tt(m8, m8t, bo, A.mult)
+    ih = al("h", 128); cp(ih, ib)
+    ihn = al("h", 128); ts(ihn, ib, -1.0, A.mult)
+    i2kh = al("h", 128); ts(i2kh, ib, 2048.0, A.mult)
+    pairh = al("h", 128); ts(pairh, bo, c_(7), A.mult)
+    mj = al("b", 128); act(mj, bo, AF.Identity, c_(9))
+    mev = al("b", 128); tmpb = al("b", 128)
+    ts(tmpb, mpar, c_(6), A.is_equal, 4096.0, A.mult); tt(mev, tmpb, bo, A.mult)
+    ipu = [al("h", 160), al("h", 160)]
+    ts(ipu[0], ipad, c_(4), A.mult); ts(ipu[1], ipad, c_(3), A.mult)
+    wl = al("f", 128); hlf = al("f", 128); zer = al("f", 128); ms(hlf, 0.5); ms(zer, 0.0)
+    scan(wl, hlf, zer, 2.0 ** 64, A.mult, A.add)
+    wd = al("f", 128); tt(wd, wl, diag, A.mult)
+    wws = al("f", 128); scan(wws, seg0, wd, 0.0, A.mult, A.add)
+    ww = sub(wws, 15, 8, 16)
+    wtd = al("f", 128); act(wtd, wd, AF.Copy, 2.5)
+    dwk = al("f", 16); ts(dwk, dw, c_(0), A.add)
+
+    cur[0] = 16
+    ms(sub(ZT, 0, 512), 0.0); ms(sub(ZT, 512, 1536), 0.0)
+    act(sub(ZT, ZW - 512, 512), sub(ZT, 0, 512), AF.Copy)
+    z0 = 2048
+    while z0 < ZV:
+        n = min(1792, ZV - z0); ms(sub(ZT, z0, n), 0.0); z0 += n
+    if ZG:
+        k = iota(sub(ZT, z0, ZG), [[0, ZG]], 0, 0); z0 += ZG
+        ops[k]["x"] = [j for j in range(k) if ops[j]["q"] == "G"]
+    while z0 < ZW - 512:
+        n = min(2048, ZW - 512 - z0); act(sub(ZT, z0, n), sub(ZT, 0, n), AF.Copy); z0 += n
+    lo_i = al("i", 1024); hi_i = al("i", 1024); lo_b = al("b", 1024); hi_b = al("b", 1024)
+    ts(lo_i, lmi, 255, A.bitwise_and); cp(lo_b, lo_i)
+    ts(hi_i, lmi, 1792, A.bitwise_and); cp(hi_b, hi_i)
+    d_z0 = dma("S", [(prt(sub(ZT, 1024 * r, 1024), r & 7, 128, 16), prt(lo_b, r, 128, 16)) for r in range(16)], 2.5)
+    d_z1 = dma("A", [(prt(sub(ZT, 1024 * r, 1024), 8 + (r & 7), 128, 16), prt(hi_b, r, 128, 16)) for r in range(16)], 2.5)
+    ops[d_z1]["w"] = [("zt2", 0, ZW, 1)]
+    ops[d_z1]["x"] = [k for k, o in enumerate(ops[:d_z0]) if any(w[0] == "zt" for w in o["w"])]
+    cur[0] = 14
+    cp(sub(RT, 0, 1024), lmi);
+    iota(sub(FD, 2048, 256), [[0, 256]], 1024, 0); iota(sub(RT, 1024, 128), [[0, 128]], 0, 0)
+    iota(sub(FWT, 2048, 256), [[0, 256]], 0, 0); iota(sub(SX, 2048, 256), [[0, 256]], 0, 0)
+    d_sn = dma("S", [(prt(sub(SX, 0, 2048), i, 128, 16), ("@sn", 0, 8, 1, 0, 2048)) for i in range(16)], 5.0)
+    d_fw = dma("S", [(sub(FWT, 0, 2048), ("@feat", 0, 128, 1, 0, 2048))], 4.0)
+    ops[d_fw]["x"].append(d_z0); ops[d_sn]["x"].append(d_z0)
+
+    L0 = "lin0"
+    s8f = al("f", 512); s8i = al("i", 256)
+    cp(prt(sub(s8f, 0, 256), 0, 8), prt(sub(sm8, 0, 256), 0, 8))
+    ts(prt(sub(s8i, 0, 128), 0, 8), prt(sub(sm8, 256, 128), 0, 8), 255, A.bitwise_and)
+    ts(prt(sub(s8i, 128, 128), 0, 8), prt(sub(sm8, 256, 128), 0, 8), 1792, A.bitwise_and)
+    cp(prt(sub(s8f, 256, 256), 0, 8), prt(s8i, 0, 8))
+    mm(sub(PS[0], 0, 256), prt(e8, 0, 8), prt(sub(s8f, 0, 256), 0, 8), True, True)
+    mm(sub(PS[0], 256, 128), prt(e8lo, 0, 8), prt(sub(s8f, 256, 128), 0, 8), True, False)
+    mm(sub(PS[0], 256, 128), prt(e8hi, 0, 8), prt(sub(s8f, 384, 128), 0, 8), False, True)
+    smd = al("f", 128); tt(smd, sub(PS[0], 0, 128), diag, A.mult)
+    cp(fld(L0, FS, 0, 128), sub(PS[0], 0, 128)); cp(fld(L0, FV, 0, 128), sub(PS[0], 256, 128))
+    thh = al("b", 128); thl = al("b", 128)
+    act(thh, sub(PS[0], 128, 128), AF.Copy); tt(thl, sub(PS[0], 128, 128), thh, A.subtract)
+    scan(fld(L0, FW, 0, 128), seg0, smd, 0.0, A.mult, A.add)
+    ts(fld(L0, FX, 0, 128), lxb, 1024.0, A.add)
+    mm(sub(PS[4], 0, 128), bo, lxb, True, True)
+    ri0 = al("i", 128); ri1 = al("i", 128)
+    ts(ri0, sub(PS[4], 0, 128), c_(0), A.add); ts(ri1, ri0, 15, A.bitwise_and); ts(fld(L0, FR, 0, 128), ri1, 1024.0, A.mult)
+    for src, f in ((lpi, FP), (lqi, FM)):
+        tf0 = al("f", 128)
+        ts(tf0, src, 0.0, A.is_lt, 4096.0, A.mult); tt(fld(L0, f, 0, 128), tf0, src, A.add)
+
+    B = {}
+    for h in range(2):
+        b = {}
+        for nm in ("G", "E", "F", "X", "G2", "E2"): b[nm] = al("b", 1024)
+        for nm in ("val", "go", "ab", "fwin"): b[nm] = al("b", 64)
+        for nm in ("cap", "n", "ny", "a1", "a2", "sm"): b[nm] = al("h", 64)
+        b["rs"] = al("h", 128); b["ct"] = al("f", 4); b["caps"] = al("f", 128)
+        for nm in ("r", "w"): b[nm] = al("f", 64)
+        for nm in ("j0", "j1"): b[nm] = al("i", 64)
+        for nm in ("o1", "o2", "on"): b[nm] = al("u", 64)
+        b["so"] = al("u", 4); b["ow"] = al("u", 8)
+        B[h] = b
+    so2 = al("u", 8); wo = al("u", 16)
+    jsel = al("b", 128); zcol = al("b", 128); notj = al("b", 128); da = al("b", 128)
+    swf = al("f", 128); jd = al("f", 128); jws = al("f", 128); rb = al("f", 128); ra = al("f", 128)
+    win = al("f", 128); wins = al("f", 128)
+    gw = al("f", 8); wgo = al("f", 8); uw = al("f", 16); uw0 = al("f", 16); uz = al("f", 8); m16 = al("f", 16); o16 = al("f", 16)
+    eqd = al("b", 1024); ac = al("f", 3); aci = al("i", 2)
+    yo = [al("f", 128) for k in range(4)]; yt = [al("f", 128), al("f", 128)]; yt2 = [al("f", 128), al("f", 128)]
+    RW, ZR = sub(RT, 0, 1024), sub(ZT, 0, 16384)
+
+    def spread(h, G):
+        for k in range(16):
+            z = mm(sub(PS[4 * h + k // 8], 64 * (k % 8), 64), bo, sub(G, k, 64, 16), True, True)
+            if k == 8: ops[z]["y"] = z - 1
+        for k in range(16):
+            y = mm(sub(PS[4 * h + 2], 0, 64), sel(0, k), sub(G, k, 64, 16), k == 0, False)
+            if k == 0: ops[y]["y"] = z
+
+    for t in range(RO):
+        LI, LO, last = "lin%d" % t, "lout%d" % t, t == RO - 1
+        cur[0] = 1
+        if t > 0:
+            tt(sub(aci, 0, 1), sub(ac, 0, 1), sub(ac, 1, 1), A.add); ts(sub(aci, 1, 1), sub(aci, 0, 1), 31, A.bitwise_and)
+            ts(sub(ac, 2, 1), sub(aci, 1, 1), -65536.0, A.mult); act(da, ib, AF.Identity, sub(ac, 2, 1))
+        for h in range(2):
+            b = B[h]; l0 = 64 * h; cur[0] = 8 * h
+            def fi(f): return fld(LI, f, l0, 64)
+            def fo(f): return fld(LO, f, l0, 64)
+            def wide(k): return sub(PS[4 * h + k // 8], 64 * (k % 8), 64)
+            sa, sb = PS[4 * h + 2], PS[4 * h + 3]
+            if t > 0:
+                for e in range(2): add("X", "arr", (t, h, e), [], [rec(LI, e, l0)], 0.0)
+            cp(b["so"], sub(fi(FW), 15, 4, 16))
+            cur[0] = 8 * h + 1
+            ts(sub(jsel, l0, 64), fi(FR), c_(1), A.is_equal)
+            xb = sub(FWT, 2048 + 2 * l0, 64, 2)
+            ts(xb, fi(FX), -1024.0, A.add); cp(sub(SX, 2048 + 2 * l0, 64, 2), fi(FS))
+            mm(sub(sb, 64, 64), mj, sub(jsel, l0, 64), True, True)
+            mm(sub(sb, 128, 64), i2kh, fi(FS), True, False); mm(sub(sb, 128, 64), pairh, fi(FV), False, True)
+            act(sub(notj, l0, 64), sub(jsel, l0, 64), AF.Identity, -1.0, 1.0)
+            if not last:
+                mm(sub(sb, 200, 64), m8, sub(jsel, l0, 64), True, True)
+                tt(sub(zcol, l0, 64), sub(sb, 200, 64), fi(FV), A.mult)
+                tt(sub(jd, l0, 64), sub(sb, 64, 64), sub(diag, l0, 64), A.mult)
+            tt(sub(rb, l0, 64), sub(sb, 128, 64), sub(jsel, l0, 64), A.mult)
+            mm(sub(sb, 0, 64), mev, sub(jsel, l0, 64), True, False); mm(sub(sb, 0, 64), ih, fi(FP), False, True)
+            tt(b["cap"], sub(sb, 0, 64), sub(selfh, l0, 64), A.min)
+            ts(b["val"], b["cap"], 2048.0, A.is_lt)
+
+            def long_gather(G, tab, off, nv):
+                na = 64 - nv; c0 = (na // 4) * 2
+                ks = [act(sub(G, 16 * a0, 16 * n), ind(tab, sub(off, a0, n)), AF.Copy) for a0, n in ((0, c0), (c0, na - c0))]
+                if nv: ks.append(cp(sub(G, 16 * na, 16 * nv), ind(tab, sub(off, na, nv))))
+                return ks
+
+            def gather_members(so, ai, ou, G, nv, pa):
+                ts(ai, ind(RW, so), 2.0 ** -11, A.mult, 1024 - 1023.5 / 2048, A.add)
+                mm(pa, ih, fi(FR), True, False); mm(pa, ih, ai, False, True)
+                ts(ou, pa, -1024.0, A.add)
+                for k in long_gather(G, ZR, ou, nv): ops[k]["x"].append(d_z1)
+
+            cur[0] = 8 * h
+            gather_members(b["so"], b["a1"], b["o1"], b["G"], GV[h][0], wide(15 * PA))
+            cur[0] = 8 * h + 2
+            spread(h, b["G"])
+            for k in range(16):
+                tt(sub(b["E"], 64 * k, 64), wide(k), fi(FM), A.is_equal)
+            mm(sub(sa, 0, 64), i4k, b["val"], False, False)
+            for k in range(16):
+                mm(sub(sa, 0, 64), sel(1, k), sub(b["E"], 64 * k, 64), False, k == 15)
+            tt(b["n"], sub(sa, 0, 64), b["cap"], A.min); cp(b["on"], b["n"]); vtr(b["ny"], b["n"])
+            cur[0] = 8 * h + 3
+            long_gather(b["F"], FD, b["on"], GV[h][1])
+            key = sub(sa, 0, 64)
+            mm(key, dk, sub(ones, 0, 64), True, False)
+            mm(key, ic, sub(thh, l0, 64), False, False); mm(key, ic, sub(thl, l0, 64), False, False)
+            if t > 0: mm(key, da, sub(ones, 0, 64), False, False)
+            if ABS[h]:
+                for k in range(16):
+                    mm(wide(k), ineg, xb, True, False); mm(wide(k), ib, sub(b["F"], k, 64, 16), False, True)
+                for c in range(2):
+                    act(sub(b["X"], 512 * c, 512), PS[4 * h + c], AF.Abs, 0.5)
+            else:
+                mm(wide(0), ib, xb, True, True)
+                mm(key, boc, xb, False, False)
+                for k in range(16):
+                    mm(key, sel(2, k), sub(b["F"], k, 64, 16), False, False)
+                for k in range(16):
+                    tt(sub(b["X"], 64 * k, 64), sub(b["F"], k, 64, 16), wide(0), A.max)
+            for k in range(16):
+                mm(key, sel(1, k), sub(b["X"], 64 * k, 64), False, k == 15)
+            ky, ke = wide(8), wide(9)
+            cur[0] = 8 * h + 4
+            vtr(ky, key)
+            scan(b["r"], segb, ky, 0.0, A.add, A.min)
+            tt(ke, ky, b["r"], A.subtract)
+            tt(b["w"], b["ny"], ke, A.subtract)
+            tt(b["ct"], sub(b["r"], 15, 4, 16), sub(selfy, l0 + 15, 4, 16), A.min)
+            scan(sub(b["rs"], 0, 64), ke, b["w"], 0.0, A.min, A.max)
+            tt(sub(b["rs"], 79, 4, 16), sub(b["rs"], 15, 4, 16), b["ct"], A.max)
+            for u in range(2):
+                for gg in range(2):
+                    mm(sub(sb, 192 + u, 4, 2), sub(ipu[u], 16 + 16 * (u - gg), 128), sub(b["rs"], 15 + 16 * gg, 4, 32), gg == 0, gg == 1)
+            cp(b["ow"], sub(sb, 192, 8))
+            tt(b["sm"], ind(sub(SX, 0, 2176 + 2 * l0), sub(b["ow"], 4, 4)), sub(diag, l0, 64), A.mult)
+            scan(sub(swf, l0, 64), sub(seg0, 0, 64), b["sm"], 0.0, A.mult, A.add)
+            cp(sub(so2, 4 * h, 4), sub(swf, l0 + 15, 4, 16))
+            gather_members(sub(so2, 4 * h, 4), b["a2"], b["o2"], b["G2"], GV[h][2], sub(sa, 64, 64))
+            cur[0] = 8 * h + 5
+            mm(wide(0), boh, b["sm"], True, True)
+            mm(wide(1), boh, b["sm"], True, False); mm(wide(1), ihn, fi(FS), False, True)
+            cp(fo(FS), wide(0))
+            act(b["ab"], wide(1), AF.Abs); act(b["go"], b["ab"], AF.Sign, 1.0, 0.0, sub(ac, h, 1))
+            if FWV: cp(b["fwin"], ind(sub(FWT, 0, 2176 + 2 * l0), sub(b["ow"], 0, 4)))
+            else: act(b["fwin"], ind(sub(FWT, 0, 2176 + 2 * l0), sub(b["ow"], 0, 4)), AF.Copy)
+            mm(sub(sb, 200, 64), ib, b["fwin"], True, False); mm(sub(sb, 200, 64), ib, xb, False, True)
+            ts(fo(FX), sub(sb, 200, 64), 0.5, A.mult, 1023.75, A.add)
+            if last:
+                ts(sub(yo[0], l0, 64), fo(FX), -1024.0, A.add); cp(sub(yo[3], l0, 64), fo(FS))
+            else:
+                cp(fo(FV), fi(FV)); cp(fo(FW), sub(swf, l0, 64))
+                mm(sub(sb, 264, 64), boh, fo(FX), True, True)
+                ts(b["j0"], sub(sb, 264, 64), c_(0), A.add, float(t + 1), A.add); ts(b["j1"], b["j0"], 15, A.bitwise_and)
+                ts(fo(FR), b["j1"], 1024.0, A.mult)
+                add("G", "send", (t, h, 0), [rec(LO, 0, l0)], [], SEND, TRAVEL)
+            for z, f in enumerate((FM, FP)):
+                mm(sub(sb, 64 * z, 64), ih, fi(f), True, False); mm(sub(sb, 64 * z, 64), i4k, b["go"], False, True)
+            act(b["caps"], sub(sb, 0, 128), AF.Copy)
+        sb = PS[5]; cur[0] = 6
+        tt(gw, sub(swf, 15, 8, 16), sub(fld(LI, FW, 0, 128), 15, 8, 16), A.not_equal); tt(wgo, gw, ww, A.mult)
+        for q in range(8):
+            ts(sub(eqd, 128 * q, 128), fld(LO, FS, 0, 128), sub(swf, 15 + 16 * q, 1), A.is_equal, sub(wgo, q, 1), A.mult)
+        for q in range(8):
+            mm(sub(sb, 328, 128), bo, sub(eqd, 128 * q, 128), q == 0, q == 7)
+        tt(sub(uw0, 0, 8), sub(swf, 15, 8, 16), sub(dwk, 0, 8), A.subtract); tt(sub(uw, 0, 8), sub(uw0, 0, 8), gw, A.mult)
+        if not last:
+            scan(jws, seg0, jd, 0.0, A.mult, A.add)
+            tt(uz, sub(swf, 15, 8, 16), sub(jws, 15, 8, 16), A.add); tt(sub(uw0, 8, 8), uz, sub(dwk, 8, 8), A.subtract)
+            tt(sub(uw, 8, 8), sub(uw0, 8, 8), gw, A.mult)
+        tt(win, sub(sb, 328, 128), wtd, A.is_lt)
+        scan(wins, seg0, win, 0.0, A.mult, A.add)
+        nw = 8 if last else 16
+        for z in range(nw // 8):
+            tt(sub(m16, 8 * z, 8), sub(wins, 15, 8, 16), sub(uw, 8 * z, 8), A.mult)
+        tt(sub(o16, 0, nw), sub(m16, 0, nw), sub(dwk, 0, nw), A.add); cp(sub(wo, 0, nw), sub(o16, 0, nw))
+        tt(ra, ind(RW, so2), notj, A.mult)
+        tt(ind(RT, sub(wo, 0, 8)), ra, rb, A.add)
+        if last:
+            dma("S", [(("@ylm", 0, 128, 1, 0, 512), sub(RT, 0, 512))], 3.0)
+            dma("A", [(("@ylm", 0, 128, 1, 512, 1024), sub(RT, 512, 512))], 3.0)
+        else:
+            cp(ind(ZT, sub(wo, 8, 8)), zcol)
+        for h in range(2):
+            b = B[h]; l0 = 64 * h; cur[0] = 8 * h + 7
+            sa, sb = sub(PS[4 * h + 2], 0, 64), sub(PS[4 * h + 3], 0, 64)
+            spread(h, b["G2"])
+            mm(sa, i4k, sub(ones, 0, 64), False, False); mm(sa, i4n, b["go"], False, False)
+            for k in range(16):
+                tt(sub(b["E2"], 64 * k, 64), sub(PS[4 * h + k // 8], 64 * (k % 8), 64), b["n"], A.is_equal)
+            mm(sb, i4k, sub(ones, 0, 64), True, False); mm(sb, i4n, b["go"], False, False); mm(sb, ih, b["n"], False, False)
+            for k in range(16):
+                mm(sa, sel(1, k), sub(b["E2"], 64 * k, 64), False, k == 15)
+                mm(sb, i4k, sub(b["E2"], 64 * k, 64), False, k == 15)
+            tt(fld(LO, FM, l0, 64), sa, sub(b["caps"], 0, 64), A.min); tt(fld(LO, FP, l0, 64), sb, sub(b["caps"], 64, 64), A.min)
+            if last:
+                for f, y in ((FP, 1), (FM, 2)):
+                    ts(sub(yt[y - 1], l0, 64), fld(LO, f, l0, 64), 2048.0, A.is_ge, -65536.0, A.mult)
+                    tt(sub(yt2[y - 1], l0, 64), sub(yt[y - 1], l0, 64), fld(LO, f, l0, 64), A.add)
+                    ts(sub(yo[y], l0, 64), sub(yt2[y - 1], l0, 64), -1.0, A.max)
+            else:
+                add("G", "send", (t, h, 1), [rec(LO, 1, l0)], [], SEND, TRAVEL)
+        if last:
+            dma("S", [(("@yx", 0, 128, 1, 0, 128), yo[0]), (("@ys", 0, 8, 1, 0, 128), prt(yo[3], 0, 128, 16))], 2.0)
+            dma("S", [(("@yp", 0, 128, 1, 0, 128), yo[1])], 2.0)
+            dma("A", [(("@yq", 0, 128, 1, 0, 128), yo[2])], 2.0)
+    return ops
+
+
+def schedule(ops):
+    n = len(ops)
+    dep = [dict() for _ in range(n)]
+    hist = {}
+    sends = {}
+    for i, o in enumerate(ops):
+        if o["k"] == "send": sends[o["a"]] = i
+        for j in o["x"]: dep[i][j] = True
+        if "y" in o: dep[i][o["y"]] = False
+        for kind, rs in (("r", o["r"]), ("w", o["w"])):
+            for (b, lo, hi, st) in rs:
+                h = hist.setdefault(b, [])
+                if b[:2] == "ps":
+                    if h and h[-1] != i: dep[i][h[-1]] = dep[i].get(h[-1], False)
+                    hist[b] = [i]
+                    if o["q"] == "P": continue
+                    b = "x" + b
+                    h = hist.setdefault(b, [])
+                for (j, kj, l2, h2, s2) in h:
+                    if j != i and l2 < hi and lo < h2 and (lo - l2) % math.gcd(st, s2) == 0 and (kind == "w" or kj == "w"):
+                        dep[i][j] = True
+        for (b, lo, hi, st) in o["w"]:
+            if b[:2] == "ps":
+                b = "x" + b
+                if o["q"] == "P":
+                    hist[b] = []
+                    continue
+            hist[b] = [e for e in hist[b] if not (lo <= e[2] and e[3] <= hi and e[4] % st == 0 and (e[2] - lo) % st == 0)] + [(i, "w", lo, hi, st)]
+        for (b, lo, hi, st) in o["r"]:
+            hist["x" + b if b[:2] == "ps" else b].append((i, "r", lo, hi, st))
+        if o["k"] == "arr": dep[i][sends[(o["a"][0] - 1, o["a"][1], o["a"][2])]] = True
+    succ = [[] for _ in range(n)]
+    for i in range(n):
+        for j in dep[i]: succ[j].append(i)
+    pr = [0.0] * n
+    for i in range(n - 1, -1, -1):
+        pr[i] = ops[i]["c"] + ops[i]["lat"] + max([pr[s] + (SYNC if ops[s]["q"] != ops[i]["q"] or dep[s][i] else 0.0) for s in succ[i]] + [0.0])
+    x = SEED
+    for i in range(n):
+        x = (x * 1103515245 + 12345) % 2147483648
+        pr[i] += NOISE * x / 2147483648 + BIAS[ops[i]["h"]]
+    left = [len(d) for d in dep]
+    rdy = [0.0] * n
+    free = {}
+    ready = [i for i in range(n) if left[i] == 0]
+    order = []
+    fin = [0.0] * n
+    if GRAIN == 0:
+        slots = {}; start = [0.0] * n
+        while ready:
+            i = max(ready, key=lambda j: (pr[j], -j))
+            ready.remove(i)
+            sl = slots.setdefault(ops[i]["q"], [])
+            st = rdy[i]; c = ops[i]["c"]; z = len(sl)
+            while z > 0 and sl[z - 1][1] > st: z -= 1
+            while z < len(sl) and sl[z][0] < st + c - 1e-9:
+                st = max(st, sl[z][1]); z += 1
+            sl.insert(z, (st, st + c))
+            start[i] = st; fin[i] = st + c + ops[i]["lat"]
+            for s in succ[i]:
+                same = ops[s]["q"] == ops[i]["q"] and not dep[s][i]
+                rdy[s] = max(rdy[s], st + c if same else fin[i] + SYNC)
+                left[s] -= 1
+                if left[s] == 0: ready.append(s)
+        order = sorted(range(n), key=lambda j: (start[j], j))
+    while ready:
+        best = None
+        for i in ready:
+            st = max(rdy[i], free.get(ops[i]["q"], 0.0))
+            key = (round(st / GRAIN), -pr[i], i)
+            if best is None or key < best[0]: best = (key, i, st)
+        i, st = best[1], best[2]
+        ready.remove(i); order.append(i)
+        free[ops[i]["q"]] = st + ops[i]["c"]
+        fin[i] = st + ops[i]["c"] + ops[i]["lat"]
+        for s in succ[i]:
+            same = ops[s]["q"] == ops[i]["q"] and not dep[s][i]
+            rdy[s] = max(rdy[s], st + ops[i]["c"] if same else fin[i] + SYNC)
+            left[s] -= 1
+            if left[s] == 0: ready.append(s)
+    prog = []
+    num = {}; idx = {}; clock = {}; know = {}; nd = 0
+    for i in order:
+        o = ops[i]; q = o["q"]
+        kn = know.setdefault(q, {})
+        waits = []
+        if o["k"] != "arr":
+            for j in sorted(dep[i], key=lambda j: -fin[j]):
+                if ops[j]["q"] == q and not dep[i][j]: continue
+                s, v = idx[j]
+                if kn.get(s, 0) >= v: continue
+                waits.append((s, v))
+                for s2, v2 in clock[j].items():
+                    if kn.get(s2, 0) < v2: kn[s2] = v2
+        if o["k"] == "dma":
+            idx[i] = ("d%d" % nd, 16 * len(o["a"])); nd += 1
+        elif o["k"] == "arr":
+            idx[i] = ("arr%d_%d_%d" % o["a"], 8)
+        elif o["k"] == "send":
+            idx[i] = ("sent", 0)
+        else:
+            num[q] = num.get(q, 0) + 1; idx[i] = ("c" + q, num[q])
+        clock[i] = dict(kn) if o["k"] != "arr" else {}
+        clock[i][idx[i][0]] = idx[i][1]
+        if o["k"] != "arr": prog.append((q, waits, o["k"], o["a"], idx[i][0]))
+    assert nd <= NDMA
+    final = {}
+    for i in order:
+        if ops[i]["k"] != "send": final[idx[i][0]] = max(final.get(idx[i][0], 0), idx[i][1])
+    final["sent"] = 8 * 4 * (RO - 1)
+    return prog, final, max(fin), ops, fin, dep, order
+
+
+CACHE = {}
+
+
+def rank_program(g, core, T, topo):
+    rank = T.rank_of(core)
+    if rank is None:
+        return
+    if "p" not in CACHE:
+        CACHE["p"] = schedule(build())
+    prog, final = CACHE["p"][0], CACHE["p"][1]
+    Q = {"V": g.vector, "A": g.scalar, "P": g.tensor, "G": g, "S": g.sync}
+
+    def ap(v):
+        if not isv(v):
+            return v
+        if v[0] == "ind":
+            return ap(v[1]).indirect(ap(v[2]))
+        if v[0][0] == "@":
+            return T[v[0][1:]][v[1]:v[2]:v[3], v[4]:v[5]]
+        return T[v[0]][v[1]:v[2]:v[3], v[4]:v[4] + (v[5] - 1) * v[6] + 1:v[6]]
+
+    for q, waits, k, a, sem in prog:
+        e = Q[q]
+        for s, v in waits:
+            e.wait_ge(T.sem[s], v)
+        if k == "dma":
+            for o, i in a:
+                e.dma_start(ap(o), ap(i)).then_inc(T.sem[sem], 16)
+            continue
+        if k == "send":
+            t, h, le = a
+            trs = []
+            for z in range(2):
+                blk = 2 * h + z
+                d = T.cores[(rank + 1 + blk) % N]
+                rid, pid = topo.addr(d, core)
+                eng = topo.engines(core, d)
+                half = len(eng) // 2
+                m = 0
+                for x in eng[z * half:(z + 1) * half]: m |= 1 << x
+                c0, c1 = blk * 32 * NFS[le], (blk + 1) * 32 * NFS[le]
+                trs.append(RemoteDMATransfer(dst_ids=[DstId(rid=rid, pnc=pid)], dma_engine_mask=m, remote_sem=T.sem["arr%d_%d_%d" % (t + 1, h, le)],
+                                             src=T["lout%d_%d" % (t, le)][:, c0:c1], dst=T["lin%d_%d" % (t + 1, le)][:, c0:c1]))
+            g.remote_dma_fused(trs, local_sem=T.sem["sent"])
+            continue
+        if k == "cp": r = e.tensor_copy(ap(a[0]), ap(a[1]))
+        elif k == "tt": r = e.tensor_tensor(ap(a[0]), ap(a[1]), ap(a[2]), a[3])
+        elif k == "ts":
+            if a[5] is None: r = e.tensor_scalar(ap(a[0]), ap(a[1]), ap(a[2]), None, a[4])
+            else: r = e.tensor_scalar(ap(a[0]), ap(a[1]), ap(a[2]), ap(a[3]), a[4], a[5])
+        elif k == "scan": r = e.tensor_tensor_scan(ap(a[0]), ap(a[1]), ap(a[2]), a[3], a[4], a[5])
+        elif k == "vtr": r = e.transpose(ap(a[0]), ap(a[1]))
+        elif k == "red": r = e.tensor_reduce(ap(a[0]), ap(a[1]), AxisListType.X, a[2])
+        elif k == "ms": r = e.memset(ap(a[0]), a[1])
+        elif k == "act":
+            if a[5] is not None: r = e.activation(ap(a[0]), ap(a[1]), a[2], accum_out=ap(a[5]))
+            elif a[4] != 0.0: r = e.activation(ap(a[0]), ap(a[1]), a[2], bias=a[4], scale=a[3])
+            elif a[3] == 1.0: r = e.activation(ap(a[0]), ap(a[1]), a[2])
+            else: r = e.activation(ap(a[0]), ap(a[1]), a[2], scale=ap(a[3]))
+        elif k == "mm": r = e.matmul(ap(a[0]), ap(a[1]), ap(a[2]), a[3], a[4])
+        elif k == "iota":
+            if a[0][0] in ("pi", "sx"): r = e.iota(ap(a[0]), a[1], a[2], a[3])
+            else: r = e.iota(ap(a[0]), a[1], a[2], a[3], allow_small_or_imprecise_dtypes=True)
+        elif k == "asel": r = e.affine_select(ap(a[0]), ap(a[1]), a[2], a[3], a[4], a[5], a[6])
+        r.then_inc(T.sem[sem], 1)
+    for s, v in final.items():
+        g.sync.wait_ge(T.sem[s], v)

@@ -3,24 +3,24 @@ from concourse.bass import DstId, RemoteDMATransfer
 from concourse.mybir import dt, AluOpType, AxisListType, ActivationFunctionType
 
 N, RO = 8, 5
-NFS = (5, 2)
-FX, FS, FV, FR, FW, FP, FM = range(7)
+NFS = (3, 2)
+FX, FW, FV, FP, FM = range(5)
 ABS = (0, 0)
-GV = ((0, 0, 0), (8, 0, 0))
-ZV, ZG = 3840, 3072
+GV = ((32, 0, 0), (32, 0, 0))
+ZV, ZG = 7424, 3072
 ZW = 16384 + 128
-PA = 0
-FWV = 0
-SEED, NOISE, GRAIN = 1, 0.0, 0.04
-BIAS = [0.5, -1.0, 1.75, -0.75, 0, 3.0, -0.25, 0.75, -0.5, 0.0, 0, 6, -0.5, -1.5, 1, -1.5, 4]
-SYNC, TRAVEL, GC, SEND = 0.1, 2.5, 1.56, 0.5
+ENG = {"so": "V", "fl": "A", "l1": "V", "o1": "A", "xb": "A", "xq": "A", "sx": "V", "sbo": "A", "on": "V", "ow": "V", "so2": "V",
+       "l2": "V", "o2": "A", "fs": "A", "lo": "A", "hi": "A", "rt": "A"}
+PASSES = 2
+GRAIN = 0.04
+BIAS = {'off0': 1, 'side0': 1.25, 'cap0': 6.75, 'nat0': 3.25, 'void0': 1.5, 'dist0': 5.75, 'min0': 0.5, 'early0': 6.0, 'new0': 6.0, 'go0': 1.25, 'late0': 0.75, 'who': 4.75, 'write': 4.5, 'table': 1.25, 'late1': -1.75, 'start': 1, 'nat1': -1.75, 'cap1': 5.5, 'side1': -0.75, 'dist1': -1.75, 'new1': -2.75, 'count': -0.75, 'feat1': -2.0, 'early1': 0.25, 'min1': -0.5, 'go1': 0.5, 'void1': 0.75}
+SYNC, TRAVEL, GC, SEND, CY = 0.2, 3.2, 1.56, 0.5, 0.00094
 
-POOL = {"b": 19456, "h": 3072, "f": 7168, "i": 5632, "u": 1024}
+POOL = {"b": 21504, "h": 4096, "f": 7168, "i": 5632, "u": 1024}
 SCRATCH = {
     "zt": ("sbuf", [128, ZW], "bfloat16"),
     "rt": ("sbuf", [128, 1152], "float32"),
     "fd": ("sbuf", [128, 2304], "bfloat16"),
-    "fw": ("sbuf", [128, 2304], "bfloat16"),
     "sx": ("sbuf", [128, 2304], "int32"),
     "pb": ("sbuf", [128, POOL["b"]], "bfloat16"),
     "ph": ("sbuf", [128, POOL["h"]], "float16"),
@@ -31,7 +31,6 @@ SCRATCH = {
 for _t in range(RO):
     for _e in range(2):
         SCRATCH["lin%d_%d" % (_t, _e)] = ("sbuf", [128, 128 * NFS[_e]], "float16")
-        SCRATCH["lout%d_%d" % (_t, _e)] = ("sbuf", [128, 128 * NFS[_e]], "float16")
 for _k in range(8):
     SCRATCH["ps%d" % _k] = ("psum", [128, 512], "float32")
 NDMA = 24
@@ -69,7 +68,7 @@ def cnt(v):
 
 def two(v):
     b = v[1][0] if v[0] == "ind" else v[0]
-    return b in WIDTH or b[:3] in ("lin", "lou")
+    return b in WIDTH or b[:3] == "lin"
 
 
 def psum(v):
@@ -78,7 +77,7 @@ def psum(v):
 
 def build():
     ops = []
-    cur = [14]
+    cur = ["start"]
     top = {"b": 0, "h": 0, "f": 0, "i": 0, "u": 0}
 
     def al(k, n):
@@ -112,36 +111,42 @@ def build():
     def vc(out, ins, tt=False):
         n = cnt(out)
         if out[0] == "ind":
-            return 0.05 + n * 3.8 * 0.00104
+            return 0.05 + n * 3.8 * CY
         if ins[0][0] == "ind":
-            return 0.05 + n * GC * 0.00104
+            return 0.05 + n * GC * CY
         f = 1.0
         if tt and not any(psum(v) for v in ins):
             f = 2.0
         elif not tt and two(out) and all(two(v) for v in ins):
             f = 0.5
-        return max(64, n * f) * 0.00104
+        return max(64, n * f) * CY
 
     def cp(o, i): return add("V", "cp", (o, i), [i], [o], vc(o, [i]))
     def tt(o, a, b, op): return add("V", "tt", (o, a, b, op), [a, b], [o], vc(o, [a, b], True))
     def ts(o, a, s1, op0, s2=None, op1=None): return add("V", "ts", (o, a, s1, s2, op0, op1), [a, s1, s2], [o], vc(o, [a]))
     def scan(o, d0, d1, init, op0, op1): return add("V", "scan", (o, d0, d1, init, op0, op1), [d0, d1], [o], vc(o, [d0, d1]))
     def vtr(o, i): return add("V", "vtr", (o, i), [i], [o], vc(o, [i]))
-    def red(o, i, op): return add("V", "red", (o, i, op), [i], [o], max(64, cnt(i)) * 0.00104)
     def ms(o, c): return add("V", "ms", (o, c), [], [o], vc(o, [o]))
     def act(o, i, f, scale=1.0, bias=0.0, acc=None):
         n = cnt(o)
-        return add("A", "act", (o, i, f, scale, bias, acc), [i, scale], [o] if acc is None else [o, acc], 0.065 + n * GC * 0.00104 if i[0] == "ind" else max(64, n) * 0.00104)
+        return add("A", "act", (o, i, f, scale, bias, acc), [i, scale, bias], [o] if acc is None else [o, acc],
+                   0.065 + n * GC * CY if i[0] == "ind" else max(64, n) * CY)
+    def lin(name, o, i, scale=1.0, bias=0.0):
+        if ENG[name] == "A":
+            return act(o, i, AF.Copy if scale == 1.0 and bias == 0.0 else AF.Identity, scale, bias)
+        if scale == 1.0 and bias == 0.0: return cp(o, i)
+        if scale == 1.0: return ts(o, i, bias, A.add)
+        return ts(o, i, scale, A.mult, bias, A.add)
     def mm(o, l, r, st, sp):
-        return add("P", "mm", (o, l, r, st, sp), [l, r], [o], max(64, cnt(r)) * 0.00052 * (1 if two(r) else 4))
-    def iota(o, pat, base, ch): return add("G", "iota", (o, pat, base, ch), [], [o], 0.13 + cnt(o) * 0.0021)
-    def asel(o, i, pat, op, fill, base, ch): return add("G", "asel", (o, i, pat, op, fill, base, ch), [i], [o], 0.17 + cnt(o) * 0.0021)
+        return add("P", "mm", (o, l, r, st, sp), [l, r], [o], max(64, cnt(r)) * CY / 2 * (1 if two(r) else 4))
+    def iota(o, pat, base, ch): return add("G", "iota", (o, pat, base, ch), [], [o], 0.13 + cnt(o) * 2 * CY)
+    def asel(o, i, pat, op, fill, base, ch): return add("G", "asel", (o, i, pat, op, fill, base, ch), [i], [o], 0.17 + cnt(o) * 2 * CY)
     def dma(q, prs, lat):
         rd = [i for o, i in prs if i[0][0] != "@"]; wr = [o for o, i in prs if o[0][0] != "@"]
         return add(q, "dma", prs, rd, wr, 0.06 * len(prs), lat)
 
     ZT, RT = vw("zt", 0, ZW), vw("rt", 0, 1152)
-    FD, FWT, SX = vw("fd", 0, 2304), vw("fw", 0, 2304), vw("sx", 0, 2304)
+    FD, SX = vw("fd", 0, 2304), vw("sx", 0, 2304)
     PS = [vw("ps%d" % k, 0, 512) for k in range(8)]
 
     def fld(buf, f, l0, n):
@@ -153,7 +158,7 @@ def build():
     dma("S", [(lmi, ("@lm", 0, 128, 1, 0, 1024))], 3.0)
     dma("S", [(lxb, ("@lx", 0, 128, 1, 0, 128)), (lpi, ("@lp", 0, 128, 1, 0, 128)), (lqi, ("@lq", 0, 128, 1, 0, 128))], 2.5)
     dma("A", [(prt(sub(sm8, 128 * k, 128), 0, 8), ("@" + nm, 0, 8, 1, 0, 128)) for k, nm in enumerate(("ls", "th", "lv"))], 2.5)
-    dma("S", [(sub(FD, 0, 2048), ("@feat", 0, 128, 1, 0, 2048))], 4.5)
+    dma("S", [(prt(sub(SX, 0, 2048), i, 128, 16), ("@sn", 0, 8, 1, 0, 2048)) for i in range(16)], 6.0)
 
     ones = al("b", 160); ms(ones, 1.0)
     ipad = al("b", 160); asel(ipad, ones, [[-1, 160]], A.is_equal, 0.0, 16, 1)
@@ -163,13 +168,19 @@ def build():
     def c_(k): return sub(col, k, 1)
     ts(sub(pi_, 1, 1), sub(pi_, 0, 1), 15, A.bitwise_and); cp(c_(0), sub(pi_, 1, 1))
     ts(sub(pi_, 2, 1), sub(pi_, 0, 1), 7, A.bitwise_and); ts(c_(1), sub(pi_, 2, 1), 2048.0, A.mult)
+    ts(c_(2), sub(pi_, 1, 1), 0.0, A.not_equal)
     ts(sub(pi_, 5, 1), sub(pi_, 0, 1), 16, A.bitwise_and); ts(c_(3), sub(pi_, 5, 1), 0.0625, A.mult)
     ts(c_(4), c_(3), -1.0, A.mult, 1.0, A.add)
     ts(sub(pi_, 6, 1), sub(pi_, 0, 1), 4, A.arith_shift_right); cp(c_(5), sub(pi_, 6, 1))
     ts(sub(pi_, 7, 1), sub(pi_, 0, 1), 1, A.bitwise_and); cp(c_(6), sub(pi_, 7, 1))
     ts(c_(7), sub(pi_, 2, 1), 0.0, A.is_equal)
-    ts(c_(8), sub(pi_, 1, 1), 4096.0, A.mult, 4096.0, A.add); ts(c_(9), sub(pi_, 1, 1), 1024.0, A.mult)
+    ts(c_(8), sub(pi_, 1, 1), 4096.0, A.mult, 4096.0, A.add); ts(c_(9), sub(pi_, 1, 1), 1024.0, A.mult, -15360.0, A.add)
     cp(c_(10), sub(pi_, 0, 1))
+    tv = al("f", 8); iota(tv, [[1, 8]], 16, 0)
+    kt = al("f", 8); ts(kt, tv, c_(0), A.add)
+    cfl = al("f", 8); ts(cfl, kt, 0.0625, A.mult, -0.46875, A.add)
+    co1 = al("f", 8); ts(co1, kt, 1024.0, A.mult, -1025.0, A.add)
+    cjs = al("f", 8); ts(cjs, kt, -1024.0, A.mult, c_(1), A.add)
     mg = al("f", 128); iota(mg, [[1, 8], [0, 16]], 0, 0)
     mk = al("f", 128); iota(mk, [[0, 8], [1, 16]], 0, 0)
     mpar = al("f", 128); iota(mpar, [[0, 64], [1, 2]], 0, 0)
@@ -178,6 +189,8 @@ def build():
     e8 = al("f", 128); e8lo = al("f", 128); e8hi = al("f", 128)
     bo = al("b", 128); ts(bo, mg, c_(5), A.is_equal)
     boh = al("h", 128); cp(boh, bo)
+    bohn = al("h", 128); ts(bohn, bo, -1.0, A.mult)
+    bo5 = al("h", 128); ts(bo5, bo, 512.0, A.mult)
     boc = al("b", 128); act(boc, bo, AF.Copy, -65536.0)
     ts(prt(e8, 0, 8), prt(mg, 0, 8), prt(c_(10), 0, 8), A.is_equal)
     t8 = al("f", 128); ts(prt(t8, 0, 8), prt(mk, 0, 8), 8.0, A.is_ge)
@@ -197,15 +210,22 @@ def build():
     dk = al("b", 128); act(dk, ib, AF.Identity, c_(8))
     i4n = al("b", 128); act(i4n, ib, AF.Copy, -4096.0)
     ic = al("b", 128); act(ic, ib, AF.Copy, -65536.0)
+    ipen = al("b", 128); act(ipen, ib, AF.Copy, 2.0 ** 29)
+    ibig = al("b", 128); act(ibig, ib, AF.Copy, 2.0 ** 70)
+    ibin = al("b", 128); act(ibin, ib, AF.Copy, -2.0 ** 70)
     m8 = al("b", 128); m8t = al("b", 128); mk8 = al("f", 128); iota(mk8, [[0, 16], [2048, 8]], 0, 0)
     ts(m8t, mk8, c_(1), A.is_equal); tt(m8, m8t, bo, A.mult)
     ih = al("h", 128); cp(ih, ib)
     ihn = al("h", 128); ts(ihn, ib, -1.0, A.mult)
     i2kh = al("h", 128); ts(i2kh, ib, 2048.0, A.mult)
+    i16n = al("h", 128); ts(i16n, ib, -16384.0, A.mult)
     pairh = al("h", 128); ts(pairh, bo, c_(7), A.mult)
+    dsh = al("h", 128); ts(dsh, sub(ipad, 17, 128), c_(2), A.mult, -1.0, A.mult)
     mj = al("b", 128); act(mj, bo, AF.Identity, c_(9))
     mev = al("b", 128); tmpb = al("b", 128)
     ts(tmpb, mpar, c_(6), A.is_equal, 4096.0, A.mult); tt(mev, tmpb, bo, A.mult)
+    mr0 = al("i", 128); mr1 = al("i", 128); mr2 = al("b", 128); mrot = al("b", 128)
+    ts(mr0, mk, c_(0), A.add, 1024.0, A.mult); ts(mr1, mr0, 15360, A.bitwise_and); cp(mr2, mr1); tt(mrot, mr2, bo, A.mult)
     ipu = [al("h", 160), al("h", 160)]
     ts(ipu[0], ipad, c_(4), A.mult); ts(ipu[1], ipad, c_(3), A.mult)
     wl = al("f", 128); hlf = al("f", 128); zer = al("f", 128); ms(hlf, 0.5); ms(zer, 0.0)
@@ -216,7 +236,7 @@ def build():
     wtd = al("f", 128); act(wtd, wd, AF.Copy, 2.5)
     dwk = al("f", 16); ts(dwk, dw, c_(0), A.add)
 
-    cur[0] = 16
+    cur[0] = "table"
     ms(sub(ZT, 0, 512), 0.0); ms(sub(ZT, 512, 1536), 0.0)
     act(sub(ZT, ZW - 512, 512), sub(ZT, 0, 512), AF.Copy)
     z0 = 2048
@@ -228,19 +248,18 @@ def build():
     while z0 < ZW - 512:
         n = min(2048, ZW - 512 - z0); act(sub(ZT, z0, n), sub(ZT, 0, n), AF.Copy); z0 += n
     lo_i = al("i", 1024); hi_i = al("i", 1024); lo_b = al("b", 1024); hi_b = al("b", 1024)
-    ts(lo_i, lmi, 255, A.bitwise_and); cp(lo_b, lo_i)
-    ts(hi_i, lmi, 1792, A.bitwise_and); cp(hi_b, hi_i)
+    ts(lo_i, lmi, 255, A.bitwise_and); lin("lo", lo_b, lo_i)
+    ts(hi_i, lmi, 1792, A.bitwise_and); lin("hi", hi_b, hi_i)
     d_z0 = dma("S", [(prt(sub(ZT, 1024 * r, 1024), r & 7, 128, 16), prt(lo_b, r, 128, 16)) for r in range(16)], 2.5)
     d_z1 = dma("A", [(prt(sub(ZT, 1024 * r, 1024), 8 + (r & 7), 128, 16), prt(hi_b, r, 128, 16)) for r in range(16)], 2.5)
     ops[d_z1]["w"] = [("zt2", 0, ZW, 1)]
     ops[d_z1]["x"] = [k for k, o in enumerate(ops[:d_z0]) if any(w[0] == "zt" for w in o["w"])]
-    cur[0] = 14
-    cp(sub(RT, 0, 1024), lmi);
-    iota(sub(FD, 2048, 256), [[0, 256]], 1024, 0); iota(sub(RT, 1024, 128), [[0, 128]], 0, 0)
-    iota(sub(FWT, 2048, 256), [[0, 256]], 0, 0); iota(sub(SX, 2048, 256), [[0, 256]], 0, 0)
-    d_sn = dma("S", [(prt(sub(SX, 0, 2048), i, 128, 16), ("@sn", 0, 8, 1, 0, 2048)) for i in range(16)], 5.0)
-    d_fw = dma("S", [(sub(FWT, 0, 2048), ("@feat", 0, 128, 1, 0, 2048))], 4.0)
-    ops[d_fw]["x"].append(d_z0); ops[d_sn]["x"].append(d_z0)
+    cur[0] = "start"
+    lin("rt", sub(RT, 0, 1024), lmi)
+    iota(sub(FD, 2048, 256), [[0, 256]], 0, 0); iota(sub(RT, 1024, 128), [[0, 128]], 0, 0)
+    iota(sub(SX, 2048, 256), [[0, 256]], 0, 0)
+    d_f = dma("S", [(sub(FD, 0, 2048), ("@feat", 0, 128, 1, 0, 2048))], 3.0)
+    ops[d_f]["y"] = d_z0
 
     L0 = "lin0"
     s8f = al("f", 512); s8i = al("i", 256)
@@ -252,14 +271,11 @@ def build():
     mm(sub(PS[0], 256, 128), prt(e8lo, 0, 8), prt(sub(s8f, 256, 128), 0, 8), True, False)
     mm(sub(PS[0], 256, 128), prt(e8hi, 0, 8), prt(sub(s8f, 384, 128), 0, 8), False, True)
     smd = al("f", 128); tt(smd, sub(PS[0], 0, 128), diag, A.mult)
-    cp(fld(L0, FS, 0, 128), sub(PS[0], 0, 128)); cp(fld(L0, FV, 0, 128), sub(PS[0], 256, 128))
+    cp(fld(L0, FV, 0, 128), sub(PS[0], 256, 128))
     thh = al("b", 128); thl = al("b", 128)
     act(thh, sub(PS[0], 128, 128), AF.Copy); tt(thl, sub(PS[0], 128, 128), thh, A.subtract)
     scan(fld(L0, FW, 0, 128), seg0, smd, 0.0, A.mult, A.add)
-    ts(fld(L0, FX, 0, 128), lxb, 1024.0, A.add)
-    mm(sub(PS[4], 0, 128), bo, lxb, True, True)
-    ri0 = al("i", 128); ri1 = al("i", 128)
-    ts(ri0, sub(PS[4], 0, 128), c_(0), A.add); ts(ri1, ri0, 15, A.bitwise_and); ts(fld(L0, FR, 0, 128), ri1, 1024.0, A.mult)
+    ts(fld(L0, FX, 0, 128), lxb, 2.0, A.mult, 2048.0, A.add)
     for src, f in ((lpi, FP), (lqi, FM)):
         tf0 = al("f", 128)
         ts(tf0, src, 0.0, A.is_lt, 4096.0, A.mult); tt(fld(L0, f, 0, 128), tf0, src, A.add)
@@ -268,86 +284,98 @@ def build():
     for h in range(2):
         b = {}
         for nm in ("G", "E", "F", "X", "G2", "E2"): b[nm] = al("b", 1024)
-        for nm in ("val", "go", "ab", "fwin"): b[nm] = al("b", 64)
-        for nm in ("cap", "n", "ny", "a1", "a2", "sm"): b[nm] = al("h", 64)
+        for nm in ("val", "ab", "c", "pen"): b[nm] = al("b", 64)
+        for nm in ("cap", "n", "n0", "a1", "a2", "sm", "fl", "sbo"): b[nm] = al("h", 64)
         b["rs"] = al("h", 128); b["ct"] = al("f", 4); b["caps"] = al("f", 128)
-        for nm in ("r", "w"): b[nm] = al("f", 64)
-        for nm in ("j0", "j1"): b[nm] = al("i", 64)
+        for nm in ("r", "dny", "xq"): b[nm] = al("f", 64)
         for nm in ("o1", "o2", "on"): b[nm] = al("u", 64)
         b["so"] = al("u", 4); b["ow"] = al("u", 8)
         B[h] = b
     so2 = al("u", 8); wo = al("u", 16)
-    jsel = al("b", 128); zcol = al("b", 128); notj = al("b", 128); da = al("b", 128)
-    swf = al("f", 128); jd = al("f", 128); jws = al("f", 128); rb = al("f", 128); ra = al("f", 128)
+    jsel = al("b", 128); zcol = al("b", 128); notj = al("b", 128); da = al("b", 128); go = al("b", 128); fsn = al("h", 128)
+    sw8 = al("f", 8); jd = al("f", 128); jws = al("f", 128); rb = al("f", 128); ra = al("f", 128)
     win = al("f", 128); wins = al("f", 128)
-    gw = al("f", 8); wgo = al("f", 8); uw = al("f", 16); uw0 = al("f", 16); uz = al("f", 8); m16 = al("f", 16); o16 = al("f", 16)
+    gw = al("f", 8); wgo = al("f", 8); uw = al("f", 16); m16 = al("f", 16); o16 = al("f", 16)
     eqd = al("b", 1024); ac = al("f", 3); aci = al("i", 2)
     yo = [al("f", 128) for k in range(4)]; yt = [al("f", 128), al("f", 128)]; yt2 = [al("f", 128), al("f", 128)]
     RW, ZR = sub(RT, 0, 1024), sub(ZT, 0, 16384)
+    LINK = (2.0 ** -11, 1025 - 1023.5 / 2048)
 
     def spread(h, G):
         for k in range(16):
             z = mm(sub(PS[4 * h + k // 8], 64 * (k % 8), 64), bo, sub(G, k, 64, 16), True, True)
             if k == 8: ops[z]["y"] = z - 1
+
+    def natural(h, G):
         for k in range(16):
-            y = mm(sub(PS[4 * h + 2], 0, 64), sel(0, k), sub(G, k, 64, 16), k == 0, False)
-            if k == 0: ops[y]["y"] = z
+            mm(sub(PS[4 * h + 2], 0, 64), sel(0, k), sub(G, k, 64, 16), k == 0, False)
+
+    def long_gather(G, tab, off, nv):
+        na = 64 - nv; c0 = (na // 4) * 2
+        ks = [act(sub(G, 16 * a0, 16 * n), ind(tab, sub(off, a0, n)), AF.Copy) for a0, n in ((0, c0), (c0, na - c0)) if n]
+        if nv: ks.append(cp(sub(G, 16 * na, 16 * nv), ind(tab, sub(off, na, nv))))
+        return ks
 
     for t in range(RO):
-        LI, LO, last = "lin%d" % t, "lout%d" % t, t == RO - 1
-        cur[0] = 1
+        LI, last = "lin%d" % t, t == RO - 1
+        cur[0] = "count"
         if t > 0:
             tt(sub(aci, 0, 1), sub(ac, 0, 1), sub(ac, 1, 1), A.add); ts(sub(aci, 1, 1), sub(aci, 0, 1), 31, A.bitwise_and)
             ts(sub(ac, 2, 1), sub(aci, 1, 1), -65536.0, A.mult); act(da, ib, AF.Identity, sub(ac, 2, 1))
         for h in range(2):
-            b = B[h]; l0 = 64 * h; cur[0] = 8 * h
+            b = B[h]; l0 = 64 * h; cur[0] = "off%d" % h
             def fi(f): return fld(LI, f, l0, 64)
-            def fo(f): return fld(LO, f, l0, 64)
             def wide(k): return sub(PS[4 * h + k // 8], 64 * (k % 8), 64)
             sa, sb = PS[4 * h + 2], PS[4 * h + 3]
+            js, gh = sub(jsel, l0, 64), sub(go, l0, 64)
             if t > 0:
                 for e in range(2): add("X", "arr", (t, h, e), [], [rec(LI, e, l0)], 0.0)
-            cp(b["so"], sub(fi(FW), 15, 4, 16))
-            cur[0] = 8 * h + 1
-            ts(sub(jsel, l0, 64), fi(FR), c_(1), A.is_equal)
-            xb = sub(FWT, 2048 + 2 * l0, 64, 2)
-            ts(xb, fi(FX), -1024.0, A.add); cp(sub(SX, 2048 + 2 * l0, 64, 2), fi(FS))
-            mm(sub(sb, 64, 64), mj, sub(jsel, l0, 64), True, True)
-            mm(sub(sb, 128, 64), i2kh, fi(FS), True, False); mm(sub(sb, 128, 64), pairh, fi(FV), False, True)
-            act(sub(notj, l0, 64), sub(jsel, l0, 64), AF.Identity, -1.0, 1.0)
+            lin("so", b["so"], sub(fi(FW), 15, 4, 16))
+            mm(wide(0), bo5, fi(FX), True, True)
+            lin("fl", b["fl"], wide(0), 2.0 ** -14, sub(cfl, t, 1))
+            lin("l1", b["a1"], ind(RW, b["so"]), LINK[0], LINK[1])
+            mm(wide(8), bo5, fi(FX), True, False); mm(wide(8), i16n, b["fl"], False, False); mm(wide(8), ih, b["a1"], False, True)
+            lin("o1", b["o1"], wide(8), 1.0, sub(co1, t, 1))
+            for k in long_gather(b["G"], ZR, b["o1"], GV[h][0]): ops[k]["x"].append(d_z1)
+            cur[0] = "side%d" % h
+            mm(sub(sa, 0, 64), bo5, fi(FX), True, False); mm(sub(sa, 0, 64), i16n, b["fl"], False, True)
+            ts(js, sub(sa, 0, 64), sub(cjs, t, 1), A.is_equal)
+            xb = sub(FD, 2048 + 2 * l0, 64, 2)
+            lin("xb", xb, fi(FX), 0.5, -1024.0); lin("xq", b["xq"], fi(FX), 0.5, 1023.5)
+            lin("sx", sub(SX, 2048 + 2 * l0, 64, 2), fi(FW))
+            mm(sub(sb, 64, 64), boh, fi(FW), True, False); mm(sub(sb, 65, 63), bohn, sub(fi(FW), 0, 63), False, False)
+            mm(sub(sb, 80, 3, 16), boh, sub(fi(FW), 15, 3, 16), False, True)
+            lin("sbo", b["sbo"], sub(sb, 64, 64))
+            act(sub(notj, l0, 64), js, AF.Identity, -1.0, 1.0)
+            mm(sub(sb, 128, 64), i2kh, b["sbo"], True, False); mm(sub(sb, 128, 64), pairh, fi(FV), False, True)
+            tt(sub(rb, l0, 64), sub(sb, 128, 64), js, A.mult)
             if not last:
-                mm(sub(sb, 200, 64), m8, sub(jsel, l0, 64), True, True)
-                tt(sub(zcol, l0, 64), sub(sb, 200, 64), fi(FV), A.mult)
-                tt(sub(jd, l0, 64), sub(sb, 64, 64), sub(diag, l0, 64), A.mult)
-            tt(sub(rb, l0, 64), sub(sb, 128, 64), sub(jsel, l0, 64), A.mult)
-            mm(sub(sb, 0, 64), mev, sub(jsel, l0, 64), True, False); mm(sub(sb, 0, 64), ih, fi(FP), False, True)
+                mm(sub(sb, 192, 64), mj, js, True, True)
+                mm(sub(sb, 256, 64), m8, js, True, True)
+                tt(sub(zcol, l0, 64), sub(sb, 256, 64), fi(FV), A.mult)
+                tt(sub(jd, l0, 64), sub(sb, 192, 64), sub(diag, l0, 64), A.mult)
+            cur[0] = "cap%d" % h
+            mm(sub(sb, 0, 64), mev, js, True, False); mm(sub(sb, 0, 64), ih, fi(FP), False, True)
+            act(b["val"], sub(sb, 0, 64), AF.Relu, -1.0, 2048.0)
             tt(b["cap"], sub(sb, 0, 64), sub(selfh, l0, 64), A.min)
-            ts(b["val"], b["cap"], 2048.0, A.is_lt)
-
-            def long_gather(G, tab, off, nv):
-                na = 64 - nv; c0 = (na // 4) * 2
-                ks = [act(sub(G, 16 * a0, 16 * n), ind(tab, sub(off, a0, n)), AF.Copy) for a0, n in ((0, c0), (c0, na - c0))]
-                if nv: ks.append(cp(sub(G, 16 * na, 16 * nv), ind(tab, sub(off, na, nv))))
-                return ks
-
-            def gather_members(so, ai, ou, G, nv, pa):
-                ts(ai, ind(RW, so), 2.0 ** -11, A.mult, 1024 - 1023.5 / 2048, A.add)
-                mm(pa, ih, fi(FR), True, False); mm(pa, ih, ai, False, True)
-                ts(ou, pa, -1024.0, A.add)
-                for k in long_gather(G, ZR, ou, nv): ops[k]["x"].append(d_z1)
-
-            cur[0] = 8 * h
-            gather_members(b["so"], b["a1"], b["o1"], b["G"], GV[h][0], wide(15 * PA))
-            cur[0] = 8 * h + 2
+            cur[0] = "nat%d" % h
+            natural(h, b["G"])
+            mm(sub(sa, 0, 64), i4k, b["val"], False, True)
+            tt(b["n0"], sub(sa, 0, 64), b["cap"], A.min); lin("on", b["on"], b["n0"])
+            cur[0] = "void%d" % h
             spread(h, b["G"])
             for k in range(16):
                 tt(sub(b["E"], 64 * k, 64), wide(k), fi(FM), A.is_equal)
-            mm(sub(sa, 0, 64), i4k, b["val"], False, False)
+            mm(sub(sb, 448, 64), ih, b["n0"], True, False)
             for k in range(16):
-                mm(sub(sa, 0, 64), sel(1, k), sub(b["E"], 64 * k, 64), False, k == 15)
-            tt(b["n"], sub(sa, 0, 64), b["cap"], A.min); cp(b["on"], b["n"]); vtr(b["ny"], b["n"])
-            cur[0] = 8 * h + 3
-            long_gather(b["F"], FD, b["on"], GV[h][1])
+                mm(sub(sb, 448, 64), sel(1, k), sub(b["E"], 64 * k, 64), False, k == 15)
+            tt(b["n"], sub(sb, 448, 64), b["cap"], A.min)
+            act(b["pen"], b["n"], AF.Relu, 1.0, -2047.0)
+            mm(sub(sb, 320, 64), ih, b["n"], True, False); mm(sub(sb, 320, 64), dsh, b["n"], False, True)
+            vtr(b["dny"], sub(sb, 320, 64))
+            cur[0] = "feat%d" % h
+            long_gather(b["F"], sub(FD, 0, 2048), b["on"], GV[h][1])
+            cur[0] = "dist%d" % h
             key = sub(sa, 0, 64)
             mm(key, dk, sub(ones, 0, 64), True, False)
             mm(key, ic, sub(thh, l0, 64), False, False); mm(key, ic, sub(thl, l0, 64), False, False)
@@ -365,61 +393,59 @@ def build():
                 for k in range(16):
                     tt(sub(b["X"], 64 * k, 64), sub(b["F"], k, 64, 16), wide(0), A.max)
             for k in range(16):
+                if k == 12: mm(key, ipen, b["pen"], False, False)
                 mm(key, sel(1, k), sub(b["X"], 64 * k, 64), False, k == 15)
-            ky, ke = wide(8), wide(9)
-            cur[0] = 8 * h + 4
+            ky = wide(8)
+            cur[0] = "min%d" % h
             vtr(ky, key)
             scan(b["r"], segb, ky, 0.0, A.add, A.min)
-            tt(ke, ky, b["r"], A.subtract)
-            tt(b["w"], b["ny"], ke, A.subtract)
+            tt(b["c"], ky, b["r"], A.not_equal)
             tt(b["ct"], sub(b["r"], 15, 4, 16), sub(selfy, l0 + 15, 4, 16), A.min)
-            scan(sub(b["rs"], 0, 64), ke, b["w"], 0.0, A.min, A.max)
+            scan(sub(b["rs"], 0, 64), b["c"], b["dny"], 0.0, A.mult, A.add)
             tt(sub(b["rs"], 79, 4, 16), sub(b["rs"], 15, 4, 16), b["ct"], A.max)
             for u in range(2):
                 for gg in range(2):
-                    mm(sub(sb, 192 + u, 4, 2), sub(ipu[u], 16 + 16 * (u - gg), 128), sub(b["rs"], 15 + 16 * gg, 4, 32), gg == 0, gg == 1)
-            cp(b["ow"], sub(sb, 192, 8))
+                    mm(sub(sb, 384 + u, 4, 2), sub(ipu[u], 16 + 16 * (u - gg), 128), sub(b["rs"], 15 + 16 * gg, 4, 32), gg == 0, gg == 1)
+            lin("ow", b["ow"], sub(sb, 384, 8))
             tt(b["sm"], ind(sub(SX, 0, 2176 + 2 * l0), sub(b["ow"], 4, 4)), sub(diag, l0, 64), A.mult)
-            scan(sub(swf, l0, 64), sub(seg0, 0, 64), b["sm"], 0.0, A.mult, A.add)
-            cp(sub(so2, 4 * h, 4), sub(swf, l0 + 15, 4, 16))
-            gather_members(sub(so2, 4 * h, 4), b["a2"], b["o2"], b["G2"], GV[h][2], sub(sa, 64, 64))
-            cur[0] = 8 * h + 5
+            scan(fi(FW), sub(seg0, 0, 64), b["sm"], 0.0, A.mult, A.add)
+            cur[0] = "early%d" % h
+            tt(fi(FX), ind(sub(FD, 0, 2176 + 2 * l0), sub(b["ow"], 0, 4)), b["xq"], A.add)
+            if not last: add("G", "send", (t, h, 0), [rec(LI, 0, l0)], [], SEND, TRAVEL)
+            cur[0] = "new%d" % h
+            lin("so2", sub(so2, 4 * h, 4), sub(fi(FW), 15, 4, 16))
+            lin("l2", b["a2"], ind(RW, sub(so2, 4 * h, 4)), LINK[0], LINK[1])
+            mm(sub(sa, 64, 64), mrot, js, True, False); mm(sub(sa, 64, 64), ih, b["a2"], False, True)
+            lin("o2", b["o2"], sub(sa, 64, 64), 1.0, -1025.0)
+            long_gather(b["G2"], ZR, b["o2"], GV[h][2])
+            cur[0] = "go%d" % h
             mm(wide(0), boh, b["sm"], True, True)
-            mm(wide(1), boh, b["sm"], True, False); mm(wide(1), ihn, fi(FS), False, True)
-            cp(fo(FS), wide(0))
-            act(b["ab"], wide(1), AF.Abs); act(b["go"], b["ab"], AF.Sign, 1.0, 0.0, sub(ac, h, 1))
-            if FWV: cp(b["fwin"], ind(sub(FWT, 0, 2176 + 2 * l0), sub(b["ow"], 0, 4)))
-            else: act(b["fwin"], ind(sub(FWT, 0, 2176 + 2 * l0), sub(b["ow"], 0, 4)), AF.Copy)
-            mm(sub(sb, 200, 64), ib, b["fwin"], True, False); mm(sub(sb, 200, 64), ib, xb, False, True)
-            ts(fo(FX), sub(sb, 200, 64), 0.5, A.mult, 1023.75, A.add)
-            if last:
-                ts(sub(yo[0], l0, 64), fo(FX), -1024.0, A.add); cp(sub(yo[3], l0, 64), fo(FS))
-            else:
-                cp(fo(FV), fi(FV)); cp(fo(FW), sub(swf, l0, 64))
-                mm(sub(sb, 264, 64), boh, fo(FX), True, True)
-                ts(b["j0"], sub(sb, 264, 64), c_(0), A.add, float(t + 1), A.add); ts(b["j1"], b["j0"], 15, A.bitwise_and)
-                ts(fo(FR), b["j1"], 1024.0, A.mult)
-                add("G", "send", (t, h, 0), [rec(LO, 0, l0)], [], SEND, TRAVEL)
+            mm(wide(1), boh, b["sm"], True, False); mm(wide(1), ihn, b["sbo"], False, True)
+            lin("fs", sub(fsn, l0, 64), wide(0))
+            if last: act(sub(yo[3], l0, 64), wide(0), AF.Copy); act(sub(yo[0], l0, 64), fi(FX), AF.Identity, 0.5, -1024.0)
+            act(b["ab"], wide(1), AF.Abs); act(gh, b["ab"], AF.Sign, 1.0, 0.0, sub(ac, h, 1))
             for z, f in enumerate((FM, FP)):
-                mm(sub(sb, 64 * z, 64), ih, fi(f), True, False); mm(sub(sb, 64 * z, 64), i4k, b["go"], False, True)
+                mm(sub(sb, 64 * z, 64), ih, fi(f), True, False); mm(sub(sb, 64 * z, 64), i4k, gh, False, True)
             act(b["caps"], sub(sb, 0, 128), AF.Copy)
-        sb = PS[5]; cur[0] = 6
-        tt(gw, sub(swf, 15, 8, 16), sub(fld(LI, FW, 0, 128), 15, 8, 16), A.not_equal); tt(wgo, gw, ww, A.mult)
+        sb = sub(PS[5], 328, 128); cur[0] = "who"
+        cp(sw8, sub(fld(LI, FW, 0, 128), 15, 8, 16))
+        tt(gw, sw8, sub(SX, 2048 + 30, 8, 32), A.not_equal); tt(wgo, gw, ww, A.mult)
         for q in range(8):
-            ts(sub(eqd, 128 * q, 128), fld(LO, FS, 0, 128), sub(swf, 15 + 16 * q, 1), A.is_equal, sub(wgo, q, 1), A.mult)
+            ts(sub(eqd, 128 * q, 128), fsn, sub(sw8, q, 1), A.is_equal, sub(wgo, q, 1), A.mult)
+        mm(sb, ibig, sub(ones, 0, 128), True, False); mm(sb, ibin, go, False, False)
         for q in range(8):
-            mm(sub(sb, 328, 128), bo, sub(eqd, 128 * q, 128), q == 0, q == 7)
-        tt(sub(uw0, 0, 8), sub(swf, 15, 8, 16), sub(dwk, 0, 8), A.subtract); tt(sub(uw, 0, 8), sub(uw0, 0, 8), gw, A.mult)
+            mm(sb, bo, sub(eqd, 128 * q, 128), False, q == 7)
+        tt(sub(uw, 0, 8), sw8, sub(dwk, 0, 8), A.subtract)
         if not last:
             scan(jws, seg0, jd, 0.0, A.mult, A.add)
-            tt(uz, sub(swf, 15, 8, 16), sub(jws, 15, 8, 16), A.add); tt(sub(uw0, 8, 8), uz, sub(dwk, 8, 8), A.subtract)
-            tt(sub(uw, 8, 8), sub(uw0, 8, 8), gw, A.mult)
-        tt(win, sub(sb, 328, 128), wtd, A.is_lt)
+            tt(sub(uw, 8, 8), sub(uw, 0, 8), sub(jws, 15, 8, 16), A.add)
+        tt(win, sb, wtd, A.is_lt)
         scan(wins, seg0, win, 0.0, A.mult, A.add)
         nw = 8 if last else 16
         for z in range(nw // 8):
             tt(sub(m16, 8 * z, 8), sub(wins, 15, 8, 16), sub(uw, 8 * z, 8), A.mult)
         tt(sub(o16, 0, nw), sub(m16, 0, nw), sub(dwk, 0, nw), A.add); cp(sub(wo, 0, nw), sub(o16, 0, nw))
+        cur[0] = "write"
         tt(ra, ind(RW, so2), notj, A.mult)
         tt(ind(RT, sub(wo, 0, 8)), ra, rb, A.add)
         if last:
@@ -428,24 +454,26 @@ def build():
         else:
             cp(ind(ZT, sub(wo, 8, 8)), zcol)
         for h in range(2):
-            b = B[h]; l0 = 64 * h; cur[0] = 8 * h + 7
+            b = B[h]; l0 = 64 * h; cur[0] = "late%d" % h
             sa, sb = sub(PS[4 * h + 2], 0, 64), sub(PS[4 * h + 3], 0, 64)
-            spread(h, b["G2"])
-            mm(sa, i4k, sub(ones, 0, 64), False, False); mm(sa, i4n, b["go"], False, False)
+            gh = sub(go, l0, 64)
+            spread(h, b["G2"]); z = len(ops) - 1
+            natural(h, b["G2"]); ops[z + 1]["y"] = z
+            mm(sa, i4k, sub(ones, 0, 64), False, False); mm(sa, i4n, gh, False, False)
             for k in range(16):
                 tt(sub(b["E2"], 64 * k, 64), sub(PS[4 * h + k // 8], 64 * (k % 8), 64), b["n"], A.is_equal)
-            mm(sb, i4k, sub(ones, 0, 64), True, False); mm(sb, i4n, b["go"], False, False); mm(sb, ih, b["n"], False, False)
+            mm(sb, i4k, sub(ones, 0, 64), True, False); mm(sb, i4n, gh, False, False); mm(sb, ih, b["n"], False, False)
             for k in range(16):
                 mm(sa, sel(1, k), sub(b["E2"], 64 * k, 64), False, k == 15)
                 mm(sb, i4k, sub(b["E2"], 64 * k, 64), False, k == 15)
-            tt(fld(LO, FM, l0, 64), sa, sub(b["caps"], 0, 64), A.min); tt(fld(LO, FP, l0, 64), sb, sub(b["caps"], 64, 64), A.min)
+            tt(fld(LI, FM, l0, 64), sa, sub(b["caps"], 0, 64), A.min); tt(fld(LI, FP, l0, 64), sb, sub(b["caps"], 64, 64), A.min)
             if last:
                 for f, y in ((FP, 1), (FM, 2)):
-                    ts(sub(yt[y - 1], l0, 64), fld(LO, f, l0, 64), 2048.0, A.is_ge, -65536.0, A.mult)
-                    tt(sub(yt2[y - 1], l0, 64), sub(yt[y - 1], l0, 64), fld(LO, f, l0, 64), A.add)
+                    ts(sub(yt[y - 1], l0, 64), fld(LI, f, l0, 64), 2048.0, A.is_ge, -65536.0, A.mult)
+                    tt(sub(yt2[y - 1], l0, 64), sub(yt[y - 1], l0, 64), fld(LI, f, l0, 64), A.add)
                     ts(sub(yo[y], l0, 64), sub(yt2[y - 1], l0, 64), -1.0, A.max)
             else:
-                add("G", "send", (t, h, 1), [rec(LO, 1, l0)], [], SEND, TRAVEL)
+                add("G", "send", (t, h, 1), [rec(LI, 1, l0)], [], SEND, TRAVEL)
         if last:
             dma("S", [(("@yx", 0, 128, 1, 0, 128), yo[0]), (("@ys", 0, 8, 1, 0, 128), prt(yo[3], 0, 128, 16))], 2.0)
             dma("S", [(("@yp", 0, 128, 1, 0, 128), yo[1])], 2.0)
@@ -453,7 +481,7 @@ def build():
     return ops
 
 
-def schedule(ops):
+def depend(ops):
     n = len(ops)
     dep = [dict() for _ in range(n)]
     hist = {}
@@ -484,40 +512,25 @@ def schedule(ops):
         for (b, lo, hi, st) in o["r"]:
             hist["x" + b if b[:2] == "ps" else b].append((i, "r", lo, hi, st))
         if o["k"] == "arr": dep[i][sends[(o["a"][0] - 1, o["a"][1], o["a"][2])]] = True
+    return dep
+
+
+def arrange0(ops, dep):
+    n = len(ops)
     succ = [[] for _ in range(n)]
     for i in range(n):
         for j in dep[i]: succ[j].append(i)
     pr = [0.0] * n
     for i in range(n - 1, -1, -1):
         pr[i] = ops[i]["c"] + ops[i]["lat"] + max([pr[s] + (SYNC if ops[s]["q"] != ops[i]["q"] or dep[s][i] else 0.0) for s in succ[i]] + [0.0])
-    x = SEED
     for i in range(n):
-        x = (x * 1103515245 + 12345) % 2147483648
-        pr[i] += NOISE * x / 2147483648 + BIAS[ops[i]["h"]]
+        pr[i] += BIAS.get(ops[i]["h"], 0.0)
     left = [len(d) for d in dep]
     rdy = [0.0] * n
     free = {}
     ready = [i for i in range(n) if left[i] == 0]
     order = []
     fin = [0.0] * n
-    if GRAIN == 0:
-        slots = {}; start = [0.0] * n
-        while ready:
-            i = max(ready, key=lambda j: (pr[j], -j))
-            ready.remove(i)
-            sl = slots.setdefault(ops[i]["q"], [])
-            st = rdy[i]; c = ops[i]["c"]; z = len(sl)
-            while z > 0 and sl[z - 1][1] > st: z -= 1
-            while z < len(sl) and sl[z][0] < st + c - 1e-9:
-                st = max(st, sl[z][1]); z += 1
-            sl.insert(z, (st, st + c))
-            start[i] = st; fin[i] = st + c + ops[i]["lat"]
-            for s in succ[i]:
-                same = ops[s]["q"] == ops[i]["q"] and not dep[s][i]
-                rdy[s] = max(rdy[s], st + c if same else fin[i] + SYNC)
-                left[s] -= 1
-                if left[s] == 0: ready.append(s)
-        order = sorted(range(n), key=lambda j: (start[j], j))
     while ready:
         best = None
         for i in ready:
@@ -533,6 +546,60 @@ def schedule(ops):
             rdy[s] = max(rdy[s], st + ops[i]["c"] if same else fin[i] + SYNC)
             left[s] -= 1
             if left[s] == 0: ready.append(s)
+    return order, fin
+
+
+def place(ops, before, after, key):
+    n = len(ops)
+    left = [len(before[i]) for i in range(n)]
+    rdy = [0.0] * n; start = [0.0] * n
+    slots = {}
+    ready = sorted([(key[i], i) for i in range(n) if left[i] == 0], reverse=True)
+    while ready:
+        i = ready.pop()[1]
+        sl = slots.setdefault(ops[i]["q"], [])
+        st = rdy[i]; c = ops[i]["c"]; z = len(sl)
+        while z > 0 and sl[z - 1][1] > st: z -= 1
+        while z < len(sl) and sl[z][0] < st + c - 1e-9:
+            st = max(st, sl[z][1]); z += 1
+        sl.insert(z, (st, st + c))
+        start[i] = st
+        new = False
+        for s, d in after[i]:
+            if rdy[s] < st + c + d: rdy[s] = st + c + d
+            left[s] -= 1
+            if left[s] == 0:
+                ready.append((key[s], s)); new = True
+        if new: ready.sort(reverse=True)
+    return start
+
+
+def arrange(ops, dep):
+    n = len(ops)
+    pre = [[] for _ in range(n)]; suc = [[] for _ in range(n)]
+    for i in range(n):
+        for j, w in dep[i].items():
+            d = ops[j]["lat"] + SYNC if (w or ops[j]["q"] != ops[i]["q"]) and ops[j]["k"] != "arr" else 0.0
+            pre[i].append((j, d)); suc[j].append((i, d))
+    tail = [0.0] * n
+    for i in range(n - 1, -1, -1):
+        tail[i] = ops[i]["c"] + max([tail[s] + d for s, d in suc[i]] + [ops[i]["lat"]])
+    key = [-tail[i] - BIAS.get(ops[i]["h"], 0.0) for i in range(n)]
+    best = None
+    for z in range(PASSES + 1):
+        start = place(ops, pre, suc, key)
+        end = max(start[i] + ops[i]["c"] + ops[i]["lat"] for i in range(n))
+        if best is None or end < best[0]: best = (end, start)
+        if z < PASSES:
+            back = place(ops, suc, pre, [-(start[i] + ops[i]["c"] + ops[i]["lat"]) for i in range(n)])
+            key = [-(back[i] + ops[i]["c"]) for i in range(n)]
+    start = best[1]
+    return sorted(range(n), key=lambda i: (start[i], i)), [start[i] + ops[i]["c"] + ops[i]["lat"] for i in range(n)]
+
+
+def schedule(ops):
+    dep = depend(ops)
+    order, fin = arrange(ops, dep)
     prog = []
     num = {}; idx = {}; clock = {}; know = {}; nd = 0
     for i in order:
@@ -563,7 +630,12 @@ def schedule(ops):
     for i in order:
         if ops[i]["k"] != "send": final[idx[i][0]] = max(final.get(idx[i][0], 0), idx[i][1])
     final["sent"] = 8 * 4 * (RO - 1)
-    return prog, final, max(fin), ops, fin, dep, order
+    return prog, final
+
+
+def send_parts(a):
+    t, h, le = a
+    return [("lin%d_%d" % (t, le), "lin%d_%d" % (t + 1, le), blk * 32 * NFS[le], (blk + 1) * 32 * NFS[le], 1 + blk) for blk in (2 * h, 2 * h + 1)]
 
 
 CACHE = {}
@@ -575,7 +647,7 @@ def rank_program(g, core, T, topo):
         return
     if "p" not in CACHE:
         CACHE["p"] = schedule(build())
-    prog, final = CACHE["p"][0], CACHE["p"][1]
+    prog, final = CACHE["p"]
     Q = {"V": g.vector, "A": g.scalar, "P": g.tensor, "G": g, "S": g.sync}
 
     def ap(v):
@@ -596,19 +668,16 @@ def rank_program(g, core, T, topo):
                 e.dma_start(ap(o), ap(i)).then_inc(T.sem[sem], 16)
             continue
         if k == "send":
-            t, h, le = a
             trs = []
-            for z in range(2):
-                blk = 2 * h + z
-                d = T.cores[(rank + 1 + blk) % N]
+            for z, (src, dst, c0, c1, ahead) in enumerate(send_parts(a)):
+                d = T.cores[(rank + ahead) % N]
                 rid, pid = topo.addr(d, core)
                 eng = topo.engines(core, d)
                 half = len(eng) // 2
                 m = 0
                 for x in eng[z * half:(z + 1) * half]: m |= 1 << x
-                c0, c1 = blk * 32 * NFS[le], (blk + 1) * 32 * NFS[le]
-                trs.append(RemoteDMATransfer(dst_ids=[DstId(rid=rid, pnc=pid)], dma_engine_mask=m, remote_sem=T.sem["arr%d_%d_%d" % (t + 1, h, le)],
-                                             src=T["lout%d_%d" % (t, le)][:, c0:c1], dst=T["lin%d_%d" % (t + 1, le)][:, c0:c1]))
+                trs.append(RemoteDMATransfer(dst_ids=[DstId(rid=rid, pnc=pid)], dma_engine_mask=m, remote_sem=T.sem["arr%d_%d_%d" % (a[0] + 1, a[1], a[2])],
+                                             src=T[src][:, c0:c1], dst=T[dst][:, c0:c1]))
             g.remote_dma_fused(trs, local_sem=T.sem["sent"])
             continue
         if k == "cp": r = e.tensor_copy(ap(a[0]), ap(a[1]))
@@ -618,11 +687,10 @@ def rank_program(g, core, T, topo):
             else: r = e.tensor_scalar(ap(a[0]), ap(a[1]), ap(a[2]), ap(a[3]), a[4], a[5])
         elif k == "scan": r = e.tensor_tensor_scan(ap(a[0]), ap(a[1]), ap(a[2]), a[3], a[4], a[5])
         elif k == "vtr": r = e.transpose(ap(a[0]), ap(a[1]))
-        elif k == "red": r = e.tensor_reduce(ap(a[0]), ap(a[1]), AxisListType.X, a[2])
         elif k == "ms": r = e.memset(ap(a[0]), a[1])
         elif k == "act":
             if a[5] is not None: r = e.activation(ap(a[0]), ap(a[1]), a[2], accum_out=ap(a[5]))
-            elif a[4] != 0.0: r = e.activation(ap(a[0]), ap(a[1]), a[2], bias=a[4], scale=a[3])
+            elif a[4] != 0.0: r = e.activation(ap(a[0]), ap(a[1]), a[2], bias=ap(a[4]), scale=ap(a[3]))
             elif a[3] == 1.0: r = e.activation(ap(a[0]), ap(a[1]), a[2])
             else: r = e.activation(ap(a[0]), ap(a[1]), a[2], scale=ap(a[3]))
         elif k == "mm": r = e.matmul(ap(a[0]), ap(a[1]), ap(a[2]), a[3], a[4])

import math
from concourse.bass import DstId, RemoteDMATransfer
from concourse.mybir import dt, AluOpType, AxisListType, ActivationFunctionType

N, RO = 8, 5
NFS = (3, 2)
FX, FW, FV, FP, FM = range(5)
ABS = (0, 0)
GV = ((32, 0, 0), (32, 0, 0))
ZV, ZG = 7424, 3072
ZW = 16384 + 128
ENG = {"so": "V", "fl": "A", "l1": "V", "o1": "A", "xb": "A", "xq": "A", "sx": "V", "sbo": "A", "on": "V", "ow": "V", "so2": "V",
       "l2": "V", "o2": "A", "fs": "A", "lo": "A", "hi": "A", "rt": "A"}
PASSES = 2
GRAIN = 0.04
BIAS = {'off0': 1, 'side0': 1.25, 'cap0': 6.75, 'nat0': 3.25, 'void0': 1.5, 'dist0': 5.75, 'min0': 0.5, 'early0': 6.0, 'new0': 6.0, 'go0': 1.25, 'late0': 0.75, 'who': 4.75, 'write': 4.5, 'table': 1.25, 'late1': -1.75, 'start': 1, 'nat1': -1.75, 'cap1': 5.5, 'side1': -0.75, 'dist1': -1.75, 'new1': -2.75, 'count': -0.75, 'feat1': -2.0, 'early1': 0.25, 'min1': -0.5, 'go1': 0.5, 'void1': 0.75}
SYNC, TRAVEL, GC, SEND, CY = 0.2, 3.2, 1.56, 0.5, 0.00094

POOL = {"b": 21504, "h": 4096, "f": 7168, "i": 5632, "u": 1024}
SCRATCH = {
    "zt": ("sbuf", [128, ZW], "bfloat16"),
    "rt": ("sbuf", [128, 1152], "float32"),
    "fd": ("sbuf", [128, 2304], "bfloat16"),
    "sx": ("sbuf", [128, 2304], "int32"),
    "pb": ("sbuf", [128, POOL["b"]], "bfloat16"),
    "ph": ("sbuf", [128, POOL["h"]], "float16"),
    "pf": ("sbuf", [128, POOL["f"]], "float32"),
    "pi": ("sbuf", [128, POOL["i"]], "int32"),
    "pu": ("sbuf", [128, POOL["u"]], "uint16"),
}
for _t in range(RO):
    for _e in range(2):
        SCRATCH["lin%d_%d" % (_t, _e)] = ("sbuf", [128, 128 * NFS[_e]], "float16")
for _k in range(8):
    SCRATCH["ps%d" % _k] = ("psum", [128, 512], "float32")
NDMA = 24
SEMAPHORES = (["cV", "cA", "cP", "cG", "sent"] + ["arr%d_%d_%d" % (t, h, e) for t in range(1, RO) for h in range(2) for e in range(2)]
              + ["d%d" % k for k in range(NDMA)])

A = AluOpType
AF = ActivationFunctionType
WIDTH = {"zt": 2, "fd": 2, "fw": 2, "pb": 2, "ph": 2, "pu": 2}


def vw(buf, c0, n, cs=1, p0=0, p1=128, ps=1):
    return (buf, p0, p1, ps, c0, n, cs)


def sub(v, a, n, cs=1):
    return (v[0], v[1], v[2], v[3], v[4] + a * v[6], n, v[6] * cs)


def prt(v, p0, p1, ps=1):
    return (v[0], p0, p1, ps, v[4], v[5], v[6])


def ind(win, off):
    return ("ind", win, off)


def isv(x):
    return isinstance(x, tuple)


def cnt(v):
    return v[2][5] * 16 if v[0] == "ind" else v[5]


def two(v):
    b = v[1][0] if v[0] == "ind" else v[0]
    return b in WIDTH or b[:3] == "lin"


def psum(v):
    return v[0][:2] == "ps"


def build():
    ops = []
    cur = ["start"]
    top = {"b": 0, "h": 0, "f": 0, "i": 0, "u": 0}

    def al(k, n):
        c0 = top[k]
        top[k] = c0 + (n + 15) // 16 * 16
        assert top[k] <= POOL[k], k
        return vw("p" + k, c0, n)

    def regs(vs):
        o = []
        for v in vs:
            if not isv(v):
                continue
            if v[0] == "ind":
                o += regs([v[1], v[2]])
            else:
                o.append((v[0], v[4], v[4] + (v[5] - 1) * v[6] + 1, v[6]))
        return o

    def add(q, k, a, rd, wr, c, lat=0.0):
        r = regs(rd)
        w = []
        for v in wr:
            if v[0] == "ind":
                w += regs([v[1]]); r += regs([v[2]])
            else:
                w += regs([v])
        ops.append({"q": q, "k": k, "a": a, "r": r, "w": w, "c": c, "lat": lat, "x": [], "h": cur[0]})
        return len(ops) - 1

    def vc(out, ins, tt=False):
        n = cnt(out)
        if out[0] == "ind":
            return 0.05 + n * 3.8 * CY
        if ins[0][0] == "ind":
            return 0.05 + n * GC * CY
        f = 1.0
        if tt and not any(psum(v) for v in ins):
            f = 2.0
        elif not tt and two(out) and all(two(v) for v in ins):
            f = 0.5
        return max(64, n * f) * CY

    def cp(o, i): return add("V", "cp", (o, i), [i], [o], vc(o, [i]))
    def tt(o, a, b, op): return add("V", "tt", (o, a, b, op), [a, b], [o], vc(o, [a, b], True))
    def ts(o, a, s1, op0, s2=None, op1=None): return add("V", "ts", (o, a, s1, s2, op0, op1), [a, s1, s2], [o], vc(o, [a]))
    def scan(o, d0, d1, init, op0, op1): return add("V", "scan", (o, d0, d1, init, op0, op1), [d0, d1], [o], vc(o, [d0, d1]))
    def vtr(o, i): return add("V", "vtr", (o, i), [i], [o], vc(o, [i]))
    def ms(o, c): return add("V", "ms", (o, c), [], [o], vc(o, [o]))
    def act(o, i, f, scale=1.0, bias=0.0, acc=None):
        n = cnt(o)
        return add("A", "act", (o, i, f, scale, bias, acc), [i, scale, bias], [o] if acc is None else [o, acc],
                   0.065 + n * GC * CY if i[0] == "ind" else max(64, n) * CY)
    def lin(name, o, i, scale=1.0, bias=0.0):
        if ENG[name] == "A":
            return act(o, i, AF.Copy if scale == 1.0 and bias == 0.0 else AF.Identity, scale, bias)
        if scale == 1.0 and bias == 0.0: return cp(o, i)
        if scale == 1.0: return ts(o, i, bias, A.add)
        return ts(o, i, scale, A.mult, bias, A.add)
    def mm(o, l, r, st, sp):
        return add("P", "mm", (o, l, r, st, sp), [l, r], [o], max(64, cnt(r)) * CY / 2 * (1 if two(r) else 4))
    def iota(o, pat, base, ch): return add("G", "iota", (o, pat, base, ch), [], [o], 0.13 + cnt(o) * 2 * CY)
    def asel(o, i, pat, op, fill, base, ch): return add("G", "asel", (o, i, pat, op, fill, base, ch), [i], [o], 0.17 + cnt(o) * 2 * CY)
    def dma(q, prs, lat):
        rd = [i for o, i in prs if i[0][0] != "@"]; wr = [o for o, i in prs if o[0][0] != "@"]
        return add(q, "dma", prs, rd, wr, 0.06 * len(prs), lat)

    ZT, RT = vw("zt", 0, ZW), vw("rt", 0, 1152)
    FD, SX = vw("fd", 0, 2304), vw("sx", 0, 2304)
    PS = [vw("ps%d" % k, 0, 512) for k in range(8)]

    def fld(buf, f, l0, n):
        e = 0 if f < NFS[0] else 1
        return vw("%s_%d" % (buf, e), l0 * NFS[e] + f - e * NFS[0], n, NFS[e])
    def rec(buf, e, l0): return vw("%s_%d" % (buf, e), l0 * NFS[e], 64 * NFS[e])

    lmi = al("i", 1024); lpi = al("i", 128); lqi = al("i", 128); sm8 = al("i", 384); lxb = al("b", 128)
    dma("S", [(lmi, ("@lm", 0, 128, 1, 0, 1024))], 3.0)
    dma("S", [(lxb, ("@lx", 0, 128, 1, 0, 128)), (lpi, ("@lp", 0, 128, 1, 0, 128)), (lqi, ("@lq", 0, 128, 1, 0, 128))], 2.5)
    dma("A", [(prt(sub(sm8, 128 * k, 128), 0, 8), ("@" + nm, 0, 8, 1, 0, 128)) for k, nm in enumerate(("ls", "th", "lv"))], 2.5)
    dma("S", [(prt(sub(SX, 0, 2048), i, 128, 16), ("@sn", 0, 8, 1, 0, 2048)) for i in range(16)], 6.0)

    ones = al("b", 160); ms(ones, 1.0)
    ipad = al("b", 160); asel(ipad, ones, [[-1, 160]], A.is_equal, 0.0, 16, 1)
    ib = sub(ipad, 16, 128)
    pi_ = al("i", 16); iota(sub(pi_, 0, 1), [[0, 1]], 0, 1)
    col = al("f", 16)
    def c_(k): return sub(col, k, 1)
    ts(sub(pi_, 1, 1), sub(pi_, 0, 1), 15, A.bitwise_and); cp(c_(0), sub(pi_, 1, 1))
    ts(sub(pi_, 2, 1), sub(pi_, 0, 1), 7, A.bitwise_and); ts(c_(1), sub(pi_, 2, 1), 2048.0, A.mult)
    ts(c_(2), sub(pi_, 1, 1), 0.0, A.not_equal)
    ts(sub(pi_, 5, 1), sub(pi_, 0, 1), 16, A.bitwise_and); ts(c_(3), sub(pi_, 5, 1), 0.0625, A.mult)
    ts(c_(4), c_(3), -1.0, A.mult, 1.0, A.add)
    ts(sub(pi_, 6, 1), sub(pi_, 0, 1), 4, A.arith_shift_right); cp(c_(5), sub(pi_, 6, 1))
    ts(sub(pi_, 7, 1), sub(pi_, 0, 1), 1, A.bitwise_and); cp(c_(6), sub(pi_, 7, 1))
    ts(c_(7), sub(pi_, 2, 1), 0.0, A.is_equal)
    ts(c_(8), sub(pi_, 1, 1), 4096.0, A.mult, 4096.0, A.add); ts(c_(9), sub(pi_, 1, 1), 1024.0, A.mult, -15360.0, A.add)
    cp(c_(10), sub(pi_, 0, 1))
    tv = al("f", 8); iota(tv, [[1, 8]], 16, 0)
    kt = al("f", 8); ts(kt, tv, c_(0), A.add)
    cfl = al("f", 8); ts(cfl, kt, 0.0625, A.mult, -0.46875, A.add)
    co1 = al("f", 8); ts(co1, kt, 1024.0, A.mult, -1025.0, A.add)
    cjs = al("f", 8); ts(cjs, kt, -1024.0, A.mult, c_(1), A.add)
    mg = al("f", 128); iota(mg, [[1, 8], [0, 16]], 0, 0)
    mk = al("f", 128); iota(mk, [[0, 8], [1, 16]], 0, 0)
    mpar = al("f", 128); iota(mpar, [[0, 64], [1, 2]], 0, 0)
    selff = al("f", 128); iota(selff, [[2, 128]], 2048, 0)
    dw = al("f", 16); iota(dw, [[15360, 2], [16, 8]], 1024, 0)
    e8 = al("f", 128); e8lo = al("f", 128); e8hi = al("f", 128)
    bo = al("b", 128); ts(bo, mg, c_(5), A.is_equal)
    boh = al("h", 128); cp(boh, bo)
    bohn = al("h", 128); ts(bohn, bo, -1.0, A.mult)
    bo5 = al("h", 128); ts(bo5, bo, 512.0, A.mult)
    boc = al("b", 128); act(boc, bo, AF.Copy, -65536.0)
    ts(prt(e8, 0, 8), prt(mg, 0, 8), prt(c_(10), 0, 8), A.is_equal)
    t8 = al("f", 128); ts(prt(t8, 0, 8), prt(mk, 0, 8), 8.0, A.is_ge)
    tt(prt(e8hi, 0, 8), prt(e8, 0, 8), prt(t8, 0, 8), A.mult); tt(prt(e8lo, 0, 8), prt(e8, 0, 8), prt(e8hi, 0, 8), A.subtract)
    sw3 = al("b", 3 * 144); ms(sw3, 0.0)
    for k, sc in enumerate((1.0, 131072.0, -65536.0)):
        act(sub(sw3, 144 * k + 16, 8, 16), sub(bo, 0, 8, 16), AF.Copy, sc)
    def sel(s, k): return sub(sw3, 144 * s + 16 - k, 128)
    diag = al("f", 128); ts(diag, mk, c_(0), A.is_equal)
    seg0 = al("f", 128); ts(seg0, mk, 0.0, A.not_equal)
    segb = al("f", 64); ts(segb, sub(mk, 0, 64), 0.0, A.is_equal, 1e12, A.mult)
    selfh = al("h", 128); cp(selfh, selff)
    selfy = al("f", 128); vtr(selfy, selff)
    i4k = al("b", 128); act(i4k, ib, AF.Copy, 4096.0)
    ineg = al("b", 128)
    if any(ABS): act(ineg, ib, AF.Copy, -1.0)
    dk = al("b", 128); act(dk, ib, AF.Identity, c_(8))
    i4n = al("b", 128); act(i4n, ib, AF.Copy, -4096.0)
    ic = al("b", 128); act(ic, ib, AF.Copy, -65536.0)
    ipen = al("b", 128); act(ipen, ib, AF.Copy, 2.0 ** 29)
    ibig = al("b", 128); act(ibig, ib, AF.Copy, 2.0 ** 70)
    ibin = al("b", 128); act(ibin, ib, AF.Copy, -2.0 ** 70)
    m8 = al("b", 128); m8t = al("b", 128); mk8 = al("f", 128); iota(mk8, [[0, 16], [2048, 8]], 0, 0)
    ts(m8t, mk8, c_(1), A.is_equal); tt(m8, m8t, bo, A.mult)
    ih = al("h", 128); cp(ih, ib)
    ihn = al("h", 128); ts(ihn, ib, -1.0, A.mult)
    i2kh = al("h", 128); ts(i2kh, ib, 2048.0, A.mult)
    i16n = al("h", 128); ts(i16n, ib, -16384.0, A.mult)
    pairh = al("h", 128); ts(pairh, bo, c_(7), A.mult)
    dsh = al("h", 128); ts(dsh, sub(ipad, 17, 128), c_(2), A.mult, -1.0, A.mult)
    mj = al("b", 128); act(mj, bo, AF.Identity, c_(9))
    mev = al("b", 128); tmpb = al("b", 128)
    ts(tmpb, mpar, c_(6), A.is_equal, 4096.0, A.mult); tt(mev, tmpb, bo, A.mult)
    mr0 = al("i", 128); mr1 = al("i", 128); mr2 = al("b", 128); mrot = al("b", 128)
    ts(mr0, mk, c_(0), A.add, 1024.0, A.mult); ts(mr1, mr0, 15360, A.bitwise_and); cp(mr2, mr1); tt(mrot, mr2, bo, A.mult)
    ipu = [al("h", 160), al("h", 160)]
    ts(ipu[0], ipad, c_(4), A.mult); ts(ipu[1], ipad, c_(3), A.mult)
    wl = al("f", 128); hlf = al("f", 128); zer = al("f", 128); ms(hlf, 0.5); ms(zer, 0.0)
    scan(wl, hlf, zer, 2.0 ** 64, A.mult, A.add)
    wd = al("f", 128); tt(wd, wl, diag, A.mult)
    wws = al("f", 128); scan(wws, seg0, wd, 0.0, A.mult, A.add)
    ww = sub(wws, 15, 8, 16)
    wtd = al("f", 128); act(wtd, wd, AF.Copy, 2.5)
    dwk = al("f", 16); ts(dwk, dw, c_(0), A.add)

    cur[0] = "table"
    ms(sub(ZT, 0, 512), 0.0); ms(sub(ZT, 512, 1536), 0.0)
    act(sub(ZT, ZW - 512, 512), sub(ZT, 0, 512), AF.Copy)
    z0 = 2048
    while z0 < ZV:
        n = min(1792, ZV - z0); ms(sub(ZT, z0, n), 0.0); z0 += n
    if ZG:
        k = iota(sub(ZT, z0, ZG), [[0, ZG]], 0, 0); z0 += ZG
        ops[k]["x"] = [j for j in range(k) if ops[j]["q"] == "G"]
    while z0 < ZW - 512:
        n = min(2048, ZW - 512 - z0); act(sub(ZT, z0, n), sub(ZT, 0, n), AF.Copy); z0 += n
    lo_i = al("i", 1024); hi_i = al("i", 1024); lo_b = al("b", 1024); hi_b = al("b", 1024)
    ts(lo_i, lmi, 255, A.bitwise_and); lin("lo", lo_b, lo_i)
    ts(hi_i, lmi, 1792, A.bitwise_and); lin("hi", hi_b, hi_i)
    d_z0 = dma("S", [(prt(sub(ZT, 1024 * r, 1024), r & 7, 128, 16), prt(lo_b, r, 128, 16)) for r in range(16)], 2.5)
    d_z1 = dma("A", [(prt(sub(ZT, 1024 * r, 1024), 8 + (r & 7), 128, 16), prt(hi_b, r, 128, 16)) for r in range(16)], 2.5)
    ops[d_z1]["w"] = [("zt2", 0, ZW, 1)]
    ops[d_z1]["x"] = [k for k, o in enumerate(ops[:d_z0]) if any(w[0] == "zt" for w in o["w"])]
    cur[0] = "start"
    lin("rt", sub(RT, 0, 1024), lmi)
    iota(sub(FD, 2048, 256), [[0, 256]], 0, 0); iota(sub(RT, 1024, 128), [[0, 128]], 0, 0)
    iota(sub(SX, 2048, 256), [[0, 256]], 0, 0)
    d_f = dma("S", [(sub(FD, 0, 2048), ("@feat", 0, 128, 1, 0, 2048))], 3.0)
    ops[d_f]["y"] = d_z0

    L0 = "lin0"
    s8f = al("f", 512); s8i = al("i", 256)
    cp(prt(sub(s8f, 0, 256), 0, 8), prt(sub(sm8, 0, 256), 0, 8))
    ts(prt(sub(s8i, 0, 128), 0, 8), prt(sub(sm8, 256, 128), 0, 8), 255, A.bitwise_and)
    ts(prt(sub(s8i, 128, 128), 0, 8), prt(sub(sm8, 256, 128), 0, 8), 1792, A.bitwise_and)
    cp(prt(sub(s8f, 256, 256), 0, 8), prt(s8i, 0, 8))
    mm(sub(PS[0], 0, 256), prt(e8, 0, 8), prt(sub(s8f, 0, 256), 0, 8), True, True)
    mm(sub(PS[0], 256, 128), prt(e8lo, 0, 8), prt(sub(s8f, 256, 128), 0, 8), True, False)
    mm(sub(PS[0], 256, 128), prt(e8hi, 0, 8), prt(sub(s8f, 384, 128), 0, 8), False, True)
    smd = al("f", 128); tt(smd, sub(PS[0], 0, 128), diag, A.mult)
    cp(fld(L0, FV, 0, 128), sub(PS[0], 256, 128))
    thh = al("b", 128); thl = al("b", 128)
    act(thh, sub(PS[0], 128, 128), AF.Copy); tt(thl, sub(PS[0], 128, 128), thh, A.subtract)
    scan(fld(L0, FW, 0, 128), seg0, smd, 0.0, A.mult, A.add)
    ts(fld(L0, FX, 0, 128), lxb, 2.0, A.mult, 2048.0, A.add)
    for src, f in ((lpi, FP), (lqi, FM)):
        tf0 = al("f", 128)
        ts(tf0, src, 0.0, A.is_lt, 4096.0, A.mult); tt(fld(L0, f, 0, 128), tf0, src, A.add)

    B = {}
    for h in range(2):
        b = {}
        for nm in ("G", "E", "F", "X", "G2", "E2"): b[nm] = al("b", 1024)
        for nm in ("val", "ab", "c", "pen"): b[nm] = al("b", 64)
        for nm in ("cap", "n", "n0", "a1", "a2", "sm", "fl", "sbo"): b[nm] = al("h", 64)
        b["rs"] = al("h", 128); b["ct"] = al("f", 4); b["caps"] = al("f", 128)
        for nm in ("r", "dny", "xq"): b[nm] = al("f", 64)
        for nm in ("o1", "o2", "on"): b[nm] = al("u", 64)
        b["so"] = al("u", 4); b["ow"] = al("u", 8)
        B[h] = b
    so2 = al("u", 8); wo = al("u", 16)
    jsel = al("b", 128); zcol = al("b", 128); notj = al("b", 128); da = al("b", 128); go = al("b", 128); fsn = al("h", 128)
    sw8 = al("f", 8); jd = al("f", 128); jws = al("f", 128); rb = al("f", 128); ra = al("f", 128)
    win = al("f", 128); wins = al("f", 128)
    gw = al("f", 8); wgo = al("f", 8); uw = al("f", 16); m16 = al("f", 16); o16 = al("f", 16)
    eqd = al("b", 1024); ac = al("f", 3); aci = al("i", 2)
    yo = [al("f", 128) for k in range(4)]; yt = [al("f", 128), al("f", 128)]; yt2 = [al("f", 128), al("f", 128)]
    RW, ZR = sub(RT, 0, 1024), sub(ZT, 0, 16384)
    LINK = (2.0 ** -11, 1025 - 1023.5 / 2048)

    def spread(h, G):
        for k in range(16):
            z = mm(sub(PS[4 * h + k // 8], 64 * (k % 8), 64), bo, sub(G, k, 64, 16), True, True)
            if k == 8: ops[z]["y"] = z - 1

    def natural(h, G):
        for k in range(16):
            mm(sub(PS[4 * h + 2], 0, 64), sel(0, k), sub(G, k, 64, 16), k == 0, False)

    def long_gather(G, tab, off, nv):
        na = 64 - nv; c0 = (na // 4) * 2
        ks = [act(sub(G, 16 * a0, 16 * n), ind(tab, sub(off, a0, n)), AF.Copy) for a0, n in ((0, c0), (c0, na - c0)) if n]
        if nv: ks.append(cp(sub(G, 16 * na, 16 * nv), ind(tab, sub(off, na, nv))))
        return ks

    for t in range(RO):
        LI, last = "lin%d" % t, t == RO - 1
        cur[0] = "count"
        if t > 0:
            tt(sub(aci, 0, 1), sub(ac, 0, 1), sub(ac, 1, 1), A.add); ts(sub(aci, 1, 1), sub(aci, 0, 1), 31, A.bitwise_and)
            ts(sub(ac, 2, 1), sub(aci, 1, 1), -65536.0, A.mult); act(da, ib, AF.Identity, sub(ac, 2, 1))
        for h in range(2):
            b = B[h]; l0 = 64 * h; cur[0] = "off%d" % h
            def fi(f): return fld(LI, f, l0, 64)
            def wide(k): return sub(PS[4 * h + k // 8], 64 * (k % 8), 64)
            sa, sb = PS[4 * h + 2], PS[4 * h + 3]
            js, gh = sub(jsel, l0, 64), sub(go, l0, 64)
            if t > 0:
                for e in range(2): add("X", "arr", (t, h, e), [], [rec(LI, e, l0)], 0.0)
            lin("so", b["so"], sub(fi(FW), 15, 4, 16))
            mm(wide(0), bo5, fi(FX), True, True)
            lin("fl", b["fl"], wide(0), 2.0 ** -14, sub(cfl, t, 1))
            lin("l1", b["a1"], ind(RW, b["so"]), LINK[0], LINK[1])
            mm(wide(8), bo5, fi(FX), True, False); mm(wide(8), i16n, b["fl"], False, False); mm(wide(8), ih, b["a1"], False, True)
            lin("o1", b["o1"], wide(8), 1.0, sub(co1, t, 1))
            for k in long_gather(b["G"], ZR, b["o1"], GV[h][0]): ops[k]["x"].append(d_z1)
            cur[0] = "side%d" % h
            mm(sub(sa, 0, 64), bo5, fi(FX), True, False); mm(sub(sa, 0, 64), i16n, b["fl"], False, True)
            ts(js, sub(sa, 0, 64), sub(cjs, t, 1), A.is_equal)
            xb = sub(FD, 2048 + 2 * l0, 64, 2)
            lin("xb", xb, fi(FX), 0.5, -1024.0); lin("xq", b["xq"], fi(FX), 0.5, 1023.5)
            lin("sx", sub(SX, 2048 + 2 * l0, 64, 2), fi(FW))
            mm(sub(sb, 64, 64), boh, fi(FW), True, False); mm(sub(sb, 65, 63), bohn, sub(fi(FW), 0, 63), False, False)
            mm(sub(sb, 80, 3, 16), boh, sub(fi(FW), 15, 3, 16), False, True)
            lin("sbo", b["sbo"], sub(sb, 64, 64))
            act(sub(notj, l0, 64), js, AF.Identity, -1.0, 1.0)
            mm(sub(sb, 128, 64), i2kh, b["sbo"], True, False); mm(sub(sb, 128, 64), pairh, fi(FV), False, True)
            tt(sub(rb, l0, 64), sub(sb, 128, 64), js, A.mult)
            if not last:
                mm(sub(sb, 192, 64), mj, js, True, True)
                mm(sub(sb, 256, 64), m8, js, True, True)
                tt(sub(zcol, l0, 64), sub(sb, 256, 64), fi(FV), A.mult)
                tt(sub(jd, l0, 64), sub(sb, 192, 64), sub(diag, l0, 64), A.mult)
            cur[0] = "cap%d" % h
            mm(sub(sb, 0, 64), mev, js, True, False); mm(sub(sb, 0, 64), ih, fi(FP), False, True)
            act(b["val"], sub(sb, 0, 64), AF.Relu, -1.0, 2048.0)
            tt(b["cap"], sub(sb, 0, 64), sub(selfh, l0, 64), A.min)
            cur[0] = "nat%d" % h
            natural(h, b["G"])
            mm(sub(sa, 0, 64), i4k, b["val"], False, True)
            tt(b["n0"], sub(sa, 0, 64), b["cap"], A.min); lin("on", b["on"], b["n0"])
            cur[0] = "void%d" % h
            spread(h, b["G"])
            for k in range(16):
                tt(sub(b["E"], 64 * k, 64), wide(k), fi(FM), A.is_equal)
            mm(sub(sb, 448, 64), ih, b["n0"], True, False)
            for k in range(16):
                mm(sub(sb, 448, 64), sel(1, k), sub(b["E"], 64 * k, 64), False, k == 15)
            tt(b["n"], sub(sb, 448, 64), b["cap"], A.min)
            act(b["pen"], b["n"], AF.Relu, 1.0, -2047.0)
            mm(sub(sb, 320, 64), ih, b["n"], True, False); mm(sub(sb, 320, 64), dsh, b["n"], False, True)
            vtr(b["dny"], sub(sb, 320, 64))
            cur[0] = "feat%d" % h
            long_gather(b["F"], sub(FD, 0, 2048), b["on"], GV[h][1])
            cur[0] = "dist%d" % h
            key = sub(sa, 0, 64)
            mm(key, dk, sub(ones, 0, 64), True, False)
            mm(key, ic, sub(thh, l0, 64), False, False); mm(key, ic, sub(thl, l0, 64), False, False)
            if t > 0: mm(key, da, sub(ones, 0, 64), False, False)
            if ABS[h]:
                for k in range(16):
                    mm(wide(k), ineg, xb, True, False); mm(wide(k), ib, sub(b["F"], k, 64, 16), False, True)
                for c in range(2):
                    act(sub(b["X"], 512 * c, 512), PS[4 * h + c], AF.Abs, 0.5)
            else:
                mm(wide(0), ib, xb, True, True)
                mm(key, boc, xb, False, False)
                for k in range(16):
                    mm(key, sel(2, k), sub(b["F"], k, 64, 16), False, False)
                for k in range(16):
                    tt(sub(b["X"], 64 * k, 64), sub(b["F"], k, 64, 16), wide(0), A.max)
            for k in range(16):
                if k == 12: mm(key, ipen, b["pen"], False, False)
                mm(key, sel(1, k), sub(b["X"], 64 * k, 64), False, k == 15)
            ky = wide(8)
            cur[0] = "min%d" % h
            vtr(ky, key)
            scan(b["r"], segb, ky, 0.0, A.add, A.min)
            tt(b["c"], ky, b["r"], A.not_equal)
            tt(b["ct"], sub(b["r"], 15, 4, 16), sub(selfy, l0 + 15, 4, 16), A.min)
            scan(sub(b["rs"], 0, 64), b["c"], b["dny"], 0.0, A.mult, A.add)
            tt(sub(b["rs"], 79, 4, 16), sub(b["rs"], 15, 4, 16), b["ct"], A.max)
            for u in range(2):
                for gg in range(2):
                    mm(sub(sb, 384 + u, 4, 2), sub(ipu[u], 16 + 16 * (u - gg), 128), sub(b["rs"], 15 + 16 * gg, 4, 32), gg == 0, gg == 1)
            lin("ow", b["ow"], sub(sb, 384, 8))
            tt(b["sm"], ind(sub(SX, 0, 2176 + 2 * l0), sub(b["ow"], 4, 4)), sub(diag, l0, 64), A.mult)
            scan(fi(FW), sub(seg0, 0, 64), b["sm"], 0.0, A.mult, A.add)
            cur[0] = "early%d" % h
            tt(fi(FX), ind(sub(FD, 0, 2176 + 2 * l0), sub(b["ow"], 0, 4)), b["xq"], A.add)
            if not last: add("G", "send", (t, h, 0), [rec(LI, 0, l0)], [], SEND, TRAVEL)
            cur[0] = "new%d" % h
            lin("so2", sub(so2, 4 * h, 4), sub(fi(FW), 15, 4, 16))
            lin("l2", b["a2"], ind(RW, sub(so2, 4 * h, 4)), LINK[0], LINK[1])
            mm(sub(sa, 64, 64), mrot, js, True, False); mm(sub(sa, 64, 64), ih, b["a2"], False, True)
            lin("o2", b["o2"], sub(sa, 64, 64), 1.0, -1025.0)
            long_gather(b["G2"], ZR, b["o2"], GV[h][2])
            cur[0] = "go%d" % h
            mm(wide(0), boh, b["sm"], True, True)
            mm(wide(1), boh, b["sm"], True, False); mm(wide(1), ihn, b["sbo"], False, True)
            lin("fs", sub(fsn, l0, 64), wide(0))
            if last: act(sub(yo[3], l0, 64), wide(0), AF.Copy); act(sub(yo[0], l0, 64), fi(FX), AF.Identity, 0.5, -1024.0)
            act(b["ab"], wide(1), AF.Abs); act(gh, b["ab"], AF.Sign, 1.0, 0.0, sub(ac, h, 1))
            for z, f in enumerate((FM, FP)):
                mm(sub(sb, 64 * z, 64), ih, fi(f), True, False); mm(sub(sb, 64 * z, 64), i4k, gh, False, True)
            act(b["caps"], sub(sb, 0, 128), AF.Copy)
        sb = sub(PS[5], 328, 128); cur[0] = "who"
        cp(sw8, sub(fld(LI, FW, 0, 128), 15, 8, 16))
        tt(gw, sw8, sub(SX, 2048 + 30, 8, 32), A.not_equal); tt(wgo, gw, ww, A.mult)
        for q in range(8):
            ts(sub(eqd, 128 * q, 128), fsn, sub(sw8, q, 1), A.is_equal, sub(wgo, q, 1), A.mult)
        mm(sb, ibig, sub(ones, 0, 128), True, False); mm(sb, ibin, go, False, False)
        for q in range(8):
            mm(sb, bo, sub(eqd, 128 * q, 128), False, q == 7)
        tt(sub(uw, 0, 8), sw8, sub(dwk, 0, 8), A.subtract)
        if not last:
            scan(jws, seg0, jd, 0.0, A.mult, A.add)
            tt(sub(uw, 8, 8), sub(uw, 0, 8), sub(jws, 15, 8, 16), A.add)
        tt(win, sb, wtd, A.is_lt)
        scan(wins, seg0, win, 0.0, A.mult, A.add)
        nw = 8 if last else 16
        for z in range(nw // 8):
            tt(sub(m16, 8 * z, 8), sub(wins, 15, 8, 16), sub(uw, 8 * z, 8), A.mult)
        tt(sub(o16, 0, nw), sub(m16, 0, nw), sub(dwk, 0, nw), A.add); cp(sub(wo, 0, nw), sub(o16, 0, nw))
        cur[0] = "write"
        tt(ra, ind(RW, so2), notj, A.mult)
        tt(ind(RT, sub(wo, 0, 8)), ra, rb, A.add)
        if last:
            dma("S", [(("@ylm", 0, 128, 1, 0, 512), sub(RT, 0, 512))], 3.0)
            dma("A", [(("@ylm", 0, 128, 1, 512, 1024), sub(RT, 512, 512))], 3.0)
        else:
            cp(ind(ZT, sub(wo, 8, 8)), zcol)
        for h in range(2):
            b = B[h]; l0 = 64 * h; cur[0] = "late%d" % h
            sa, sb = sub(PS[4 * h + 2], 0, 64), sub(PS[4 * h + 3], 0, 64)
            gh = sub(go, l0, 64)
            spread(h, b["G2"]); z = len(ops) - 1
            natural(h, b["G2"]); ops[z + 1]["y"] = z
            mm(sa, i4k, sub(ones, 0, 64), False, False); mm(sa, i4n, gh, False, False)
            for k in range(16):
                tt(sub(b["E2"], 64 * k, 64), sub(PS[4 * h + k // 8], 64 * (k % 8), 64), b["n"], A.is_equal)
            mm(sb, i4k, sub(ones, 0, 64), True, False); mm(sb, i4n, gh, False, False); mm(sb, ih, b["n"], False, False)
            for k in range(16):
                mm(sa, sel(1, k), sub(b["E2"], 64 * k, 64), False, k == 15)
                mm(sb, i4k, sub(b["E2"], 64 * k, 64), False, k == 15)
            tt(fld(LI, FM, l0, 64), sa, sub(b["caps"], 0, 64), A.min); tt(fld(LI, FP, l0, 64), sb, sub(b["caps"], 64, 64), A.min)
            if last:
                for f, y in ((FP, 1), (FM, 2)):
                    ts(sub(yt[y - 1], l0, 64), fld(LI, f, l0, 64), 2048.0, A.is_ge, -65536.0, A.mult)
                    tt(sub(yt2[y - 1], l0, 64), sub(yt[y - 1], l0, 64), fld(LI, f, l0, 64), A.add)
                    ts(sub(yo[y], l0, 64), sub(yt2[y - 1], l0, 64), -1.0, A.max)
            else:
                add("G", "send", (t, h, 1), [rec(LI, 1, l0)], [], SEND, TRAVEL)
        if last:
            dma("S", [(("@yx", 0, 128, 1, 0, 128), yo[0]), (("@ys", 0, 8, 1, 0, 128), prt(yo[3], 0, 128, 16))], 2.0)
            dma("S", [(("@yp", 0, 128, 1, 0, 128), yo[1])], 2.0)
            dma("A", [(("@yq", 0, 128, 1, 0, 128), yo[2])], 2.0)
    return ops


def depend(ops):
    n = len(ops)
    dep = [dict() for _ in range(n)]
    hist = {}
    sends = {}
    for i, o in enumerate(ops):
        if o["k"] == "send": sends[o["a"]] = i
        for j in o["x"]: dep[i][j] = True
        if "y" in o: dep[i][o["y"]] = False
        for kind, rs in (("r", o["r"]), ("w", o["w"])):
            for (b, lo, hi, st) in rs:
                h = hist.setdefault(b, [])
                if b[:2] == "ps":
                    if h and h[-1] != i: dep[i][h[-1]] = dep[i].get(h[-1], False)
                    hist[b] = [i]
                    if o["q"] == "P": continue
                    b = "x" + b
                    h = hist.setdefault(b, [])
                for (j, kj, l2, h2, s2) in h:
                    if j != i and l2 < hi and lo < h2 and (lo - l2) % math.gcd(st, s2) == 0 and (kind == "w" or kj == "w"):
                        dep[i][j] = True
        for (b, lo, hi, st) in o["w"]:
            if b[:2] == "ps":
                b = "x" + b
                if o["q"] == "P":
                    hist[b] = []
                    continue
            hist[b] = [e for e in hist[b] if not (lo <= e[2] and e[3] <= hi and e[4] % st == 0 and (e[2] - lo) % st == 0)] + [(i, "w", lo, hi, st)]
        for (b, lo, hi, st) in o["r"]:
            hist["x" + b if b[:2] == "ps" else b].append((i, "r", lo, hi, st))
        if o["k"] == "arr": dep[i][sends[(o["a"][0] - 1, o["a"][1], o["a"][2])]] = True
    return dep


def arrange0(ops, dep):
    n = len(ops)
    succ = [[] for _ in range(n)]
    for i in range(n):
        for j in dep[i]: succ[j].append(i)
    pr = [0.0] * n
    for i in range(n - 1, -1, -1):
        pr[i] = ops[i]["c"] + ops[i]["lat"] + max([pr[s] + (SYNC if ops[s]["q"] != ops[i]["q"] or dep[s][i] else 0.0) for s in succ[i]] + [0.0])
    for i in range(n):
        pr[i] += BIAS.get(ops[i]["h"], 0.0)
    left = [len(d) for d in dep]
    rdy = [0.0] * n
    free = {}
    ready = [i for i in range(n) if left[i] == 0]
    order = []
    fin = [0.0] * n
    while ready:
        best = None
        for i in ready:
            st = max(rdy[i], free.get(ops[i]["q"], 0.0))
            key = (round(st / GRAIN), -pr[i], i)
            if best is None or key < best[0]: best = (key, i, st)
        i, st = best[1], best[2]
        ready.remove(i); order.append(i)
        free[ops[i]["q"]] = st + ops[i]["c"]
        fin[i] = st + ops[i]["c"] + ops[i]["lat"]
        for s in succ[i]:
            same = ops[s]["q"] == ops[i]["q"] and not dep[s][i]
            rdy[s] = max(rdy[s], st + ops[i]["c"] if same else fin[i] + SYNC)
            left[s] -= 1
            if left[s] == 0: ready.append(s)
    return order, fin


def place(ops, before, after, key):
    n = len(ops)
    left = [len(before[i]) for i in range(n)]
    rdy = [0.0] * n; start = [0.0] * n
    slots = {}
    ready = sorted([(key[i], i) for i in range(n) if left[i] == 0], reverse=True)
    while ready:
        i = ready.pop()[1]
        sl = slots.setdefault(ops[i]["q"], [])
        st = rdy[i]; c = ops[i]["c"]; z = len(sl)
        while z > 0 and sl[z - 1][1] > st: z -= 1
        while z < len(sl) and sl[z][0] < st + c - 1e-9:
            st = max(st, sl[z][1]); z += 1
        sl.insert(z, (st, st + c))
        start[i] = st
        new = False
        for s, d in after[i]:
            if rdy[s] < st + c + d: rdy[s] = st + c + d
            left[s] -= 1
            if left[s] == 0:
                ready.append((key[s], s)); new = True
        if new: ready.sort(reverse=True)
    return start


def arrange(ops, dep):
    n = len(ops)
    pre = [[] for _ in range(n)]; suc = [[] for _ in range(n)]
    for i in range(n):
        for j, w in dep[i].items():
            d = ops[j]["lat"] + SYNC if (w or ops[j]["q"] != ops[i]["q"]) and ops[j]["k"] != "arr" else 0.0
            pre[i].append((j, d)); suc[j].append((i, d))
    tail = [0.0] * n
    for i in range(n - 1, -1, -1):
        tail[i] = ops[i]["c"] + max([tail[s] + d for s, d in suc[i]] + [ops[i]["lat"]])
    key = [-tail[i] - BIAS.get(ops[i]["h"], 0.0) for i in range(n)]
    best = None
    for z in range(PASSES + 1):
        start = place(ops, pre, suc, key)
        end = max(start[i] + ops[i]["c"] + ops[i]["lat"] for i in range(n))
        if best is None or end < best[0]: best = (end, start)
        if z < PASSES:
            back = place(ops, suc, pre, [-(start[i] + ops[i]["c"] + ops[i]["lat"]) for i in range(n)])
            key = [-(back[i] + ops[i]["c"]) for i in range(n)]
    start = best[1]
    return sorted(range(n), key=lambda i: (start[i], i)), [start[i] + ops[i]["c"] + ops[i]["lat"] for i in range(n)]


def schedule(ops):
    dep = depend(ops)
    order, fin = arrange(ops, dep)
    prog = []
    num = {}; idx = {}; clock = {}; know = {}; nd = 0
    for i in order:
        o = ops[i]; q = o["q"]
        kn = know.setdefault(q, {})
        waits = []
        if o["k"] != "arr":
            for j in sorted(dep[i], key=lambda j: -fin[j]):
                if ops[j]["q"] == q and not dep[i][j]: continue
                s, v = idx[j]
                if kn.get(s, 0) >= v: continue
                waits.append((s, v))
                for s2, v2 in clock[j].items():
                    if kn.get(s2, 0) < v2: kn[s2] = v2
        if o["k"] == "dma":
            idx[i] = ("d%d" % nd, 16 * len(o["a"])); nd += 1
        elif o["k"] == "arr":
            idx[i] = ("arr%d_%d_%d" % o["a"], 8)
        elif o["k"] == "send":
            idx[i] = ("sent", 0)
        else:
            num[q] = num.get(q, 0) + 1; idx[i] = ("c" + q, num[q])
        clock[i] = dict(kn) if o["k"] != "arr" else {}
        clock[i][idx[i][0]] = idx[i][1]
        if o["k"] != "arr": prog.append((q, waits, o["k"], o["a"], idx[i][0]))
    assert nd <= NDMA
    final = {}
    for i in order:
        if ops[i]["k"] != "send": final[idx[i][0]] = max(final.get(idx[i][0], 0), idx[i][1])
    final["sent"] = 8 * 4 * (RO - 1)
    return prog, final


def send_parts(a):
    t, h, le = a
    return [("lin%d_%d" % (t, le), "lin%d_%d" % (t + 1, le), blk * 32 * NFS[le], (blk + 1) * 32 * NFS[le], 1 + blk) for blk in (2 * h, 2 * h + 1)]


CACHE = {}


def rank_program(g, core, T, topo):
    rank = T.rank_of(core)
    if rank is None:
        return
    if "p" not in CACHE:
        CACHE["p"] = schedule(build())
    prog, final = CACHE["p"]
    Q = {"V": g.vector, "A": g.scalar, "P": g.tensor, "G": g, "S": g.sync}

    def ap(v):
        if not isv(v):
            return v
        if v[0] == "ind":
            return ap(v[1]).indirect(ap(v[2]))
        if v[0][0] == "@":
            return T[v[0][1:]][v[1]:v[2]:v[3], v[4]:v[5]]
        return T[v[0]][v[1]:v[2]:v[3], v[4]:v[4] + (v[5] - 1) * v[6] + 1:v[6]]

    for q, waits, k, a, sem in prog:
        e = Q[q]
        for s, v in waits:
            e.wait_ge(T.sem[s], v)
        if k == "dma":
            for o, i in a:
                e.dma_start(ap(o), ap(i)).then_inc(T.sem[sem], 16)
            continue
        if k == "send":
            trs = []
            for z, (src, dst, c0, c1, ahead) in enumerate(send_parts(a)):
                d = T.cores[(rank + ahead) % N]
                rid, pid = topo.addr(d, core)
                eng = topo.engines(core, d)
                half = len(eng) // 2
                m = 0
                for x in eng[z * half:(z + 1) * half]: m |= 1 << x
                trs.append(RemoteDMATransfer(dst_ids=[DstId(rid=rid, pnc=pid)], dma_engine_mask=m, remote_sem=T.sem["arr%d_%d_%d" % (a[0] + 1, a[1], a[2])],
                                             src=T[src][:, c0:c1], dst=T[dst][:, c0:c1]))
            g.remote_dma_fused(trs, local_sem=T.sem["sent"])
            continue
        if k == "cp": r = e.tensor_copy(ap(a[0]), ap(a[1]))
        elif k == "tt": r = e.tensor_tensor(ap(a[0]), ap(a[1]), ap(a[2]), a[3])
        elif k == "ts":
            if a[5] is None: r = e.tensor_scalar(ap(a[0]), ap(a[1]), ap(a[2]), None, a[4])
            else: r = e.tensor_scalar(ap(a[0]), ap(a[1]), ap(a[2]), ap(a[3]), a[4], a[5])
        elif k == "scan": r = e.tensor_tensor_scan(ap(a[0]), ap(a[1]), ap(a[2]), a[3], a[4], a[5])
        elif k == "vtr": r = e.transpose(ap(a[0]), ap(a[1]))
        elif k == "ms": r = e.memset(ap(a[0]), a[1])
        elif k == "act":
            if a[5] is not None: r = e.activation(ap(a[0]), ap(a[1]), a[2], accum_out=ap(a[5]))
            elif a[4] != 0.0: r = e.activation(ap(a[0]), ap(a[1]), a[2], bias=ap(a[4]), scale=ap(a[3]))
            elif a[3] == 1.0: r = e.activation(ap(a[0]), ap(a[1]), a[2])
            else: r = e.activation(ap(a[0]), ap(a[1]), a[2], scale=ap(a[3]))
        elif k == "mm": r = e.matmul(ap(a[0]), ap(a[1]), ap(a[2]), a[3], a[4])
        elif k == "iota":
            if a[0][0] in ("pi", "sx"): r = e.iota(ap(a[0]), a[1], a[2], a[3])
            else: r = e.iota(ap(a[0]), a[1], a[2], a[3], allow_small_or_imprecise_dtypes=True)
        elif k == "asel": r = e.affine_select(ap(a[0]), ap(a[1]), a[2], a[3], a[4], a[5], a[6])
        r.then_inc(T.sem[sem], 1)
    for s, v in final.items():
        g.sync.wait_ge(T.sem[s], v)
